import numpy as np
import ml_dtypes


def mxq(x, axis, fmt="e4m3"):
    dtype, down = {"e4m3": (ml_dtypes.float8_e4m3fn, 7), "e5m2": (ml_dtypes.float8_e5m2, 14)}[fmt]
    v = np.moveaxis(np.asarray(x, np.float32).astype(ml_dtypes.bfloat16).astype(np.float64), axis, -1)
    blocks = v.reshape(v.shape[:-1] + (-1, 32))
    amax = np.abs(blocks).max(-1, keepdims=True)
    byte = np.maximum(np.where(amax > 0, np.frexp(amax)[1] - 1 + 127, 0) - down, 1)
    scale = np.exp2(byte - 127.0)
    codes = (blocks / scale).astype(np.float32).astype(dtype).astype(np.float64)
    return np.moveaxis((codes * scale).reshape(v.shape), -1, axis)


WIDE = False


def mx_kscale(k):
    if not WIDE:
        return np.ones(k)
    levels = np.array([10, -10, 5, -5, 0])
    if k % 512:
        return np.exp2(np.random.permutation(np.resize(levels, k // 32))).repeat(32)
    a = np.empty((k // 512, 16))
    for p in range(k // 512):
        a[p, :8] = np.random.permutation(np.resize(levels, 8))
        for g in range(8):
            far = levels[np.abs(levels - a[p, g]) >= 10]
            a[p, g + 8] = far[np.random.randint(len(far))]
    return np.exp2(a.ravel()).repeat(32)


def f64(x):
    return np.asarray(x).astype(np.float64)


def striped(idx):
    return np.tile(idx.reshape(-1, 16).T, (8, 1)).astype(np.uint16)


def unstriped(offs):
    return offs[:16].T.reshape(-1).astype(np.int64)


E2M1 = np.array([0.0, 0.5, 1.0, 1.5, 2.0, 3.0, 4.0, 6.0, -0.0, -0.5, -1.0, -1.5, -2.0, -3.0, -4.0, -6.0])


def pack_weight(w, fmt):
    k, n = w.shape
    w = f64(np.asarray(w, np.float32).astype(ml_dtypes.bfloat16)).reshape(k // 32, 32, n)
    amax = np.abs(w).max(1)
    if fmt == "e4m3":
        byte = np.frexp(amax)[1] - 1 + 127 - 7
    else:
        mant, ex = np.frexp(amax / 6.0)
        byte = np.where(mant > 0.5, ex, ex - 1) + 127
    byte = np.clip(np.where(amax > 0, byte, 1), 1, 254)
    scaled = (w * np.exp2(127.0 - byte)[:, None, :]).reshape(k, n).astype(np.float32)
    by_word = np.ascontiguousarray(scaled.reshape(k // 512, 128, 4, n).transpose(0, 1, 3, 2))
    if fmt == "e4m3":
        words = by_word.astype(ml_dtypes.float8_e4m3fn).view(np.uint8)
    else:
        c = by_word.astype(ml_dtypes.float4_e2m1fn).view(np.uint8) & 0xF
        words = (c[..., 0::2] | (c[..., 1::2] << 4)).reshape(k // 512, 128, 2 * n)
    return np.ascontiguousarray(words), np.ascontiguousarray(byte.astype(np.uint8).reshape(k // 512, 16, n))


def unpack_weight(words, scales, fmt):
    g, _, n = scales.shape
    words = np.ascontiguousarray(words).reshape(g, 128, n, -1)
    if fmt == "e4m3":
        vals = words.view(ml_dtypes.float8_e4m3fn).astype(np.float64)
    else:
        nib = np.empty((g, 128, n, 4), np.uint8)
        nib[..., 0::2] = words & 0xF
        nib[..., 1::2] = words >> 4
        vals = E2M1[nib]
    vals = vals * np.repeat(np.exp2(scales.astype(np.float64) - 127.0), 8, axis=1)[..., None]
    return vals.transpose(0, 1, 3, 2).reshape(g * 512, n)


def gelu(v):
    return 0.5 * v * (1.0 + np.tanh(np.sqrt(2.0 / np.pi) * (v + 0.044715 * v**3)))


K, T, S, T2, S2, SO, N = 1024, 4096, 1024, 2048, 1024, 512, 512

def setup_inputs():
    n = np.random.standard_normal
    s = mx_kscale(K)[:, None]
    u = mx_kscale(S)
    tab_words, tab_scales = pack_weight(n((K, T)) * s, "e4m3")
    tab2_words, tab2_scales = pack_weight(0.7 * n((K, T2)) / np.sqrt(K) / s, "e4m3")
    w = n((S, N)) / np.sqrt(S) / u[:, None]
    w4_words, w4_scales = pack_weight(w[:SO], "e2m1")
    return {
        "tab_words": tab_words, "tab_scales": tab_scales,
        "tab2_words": tab2_words, "tab2_scales": tab2_scales,
        "offs": striped(np.random.permutation(T)[:S]),
        "offs2": striped(np.random.permutation(T2)[:S2]),
        "fw": (np.exp(0.3 * n(S)) * u).astype(np.float32),
        "w4_words": w4_words, "w4_scales": w4_scales,
        "wn": w[SO:].astype(np.float32),
        "base": n(N).astype(np.float32),
    }

def reference(tab_words, tab_scales, tab2_words, tab2_scales, offs, offs2, fw, w4_words, w4_scales, wn, base):
    v = unpack_weight(tab_words, tab_scales, "e4m3")[:, unstriped(offs)]
    v2 = unpack_weight(tab2_words, tab2_scales, "e4m3")[:, unstriped(offs2)]
    a = v.T @ v2
    z = np.square(a + 1.0) * f64(fw)[:, None]
    zq = mxq(z, 0, "e4m3")
    w4 = unpack_weight(w4_words, w4_scales, "e2m1")
    wq = mxq(f64(wn), 0, "e4m3")
    y = w4.T @ zq[:SO] + wq.T @ zq[SO:]
    return y + f64(base)[:, None]

@@ -1,0 +1,212 @@
+from contextlib import ExitStack
+
+import concourse.mybir as mybir
+
+K, T, S, T2, S2, SO, N = 1024, 4096, 1024, 2048, 1024, 512, 512
+FLOPS = 2 * K * S * S2 + 2 * S * N * S2
+
+F32 = mybir.dt.float32
+BF16 = mybir.dt.bfloat16
+I32 = mybir.dt.int32
+U32 = mybir.dt.uint32
+U16 = mybir.dt.uint16
+U8 = mybir.dt.uint8
+FP8X4 = mybir.dt.float8_e4m3fn_x4
+FP4X4 = mybir.dt.float4_e2m1fn_x4
+ACT = mybir.ActivationFunctionType
+ALU = mybir.AluOpType
+
+P = 128
+PACK = 4
+KP = P * PACK
+JW = 512
+RUN = 4
+FRAG_ROW = (0, 4)
+ASSAY_ROW = (8, 12)
+
+
+def tile_list_fragment_assay_screen_kernel(
+    tc, tab_words, tab_scales, tab2_words, tab2_scales, offs, offs2, fw, w4_words, w4_scales, wn, base, out
+):
+    nc = tc.nc
+    with ExitStack() as ctx:
+        keep = ctx.enter_context(tc.tile_pool(name="keep", bufs=1))
+        ring = ctx.enter_context(tc.tile_pool(name="ring", bufs=3))
+        psum = ctx.enter_context(tc.psum_pool(name="psum", bufs=8))
+
+        frag_list = keep.tile([P, S // 16], U16, name="frag_list")
+        assay_list = keep.tile([P, S2 // 16], U16, name="assay_list")
+        frag_tab = [keep.tile([P, T], I32, name="frag_tab%d" % a, align_bytes=64) for a in range(2)]
+        assay_tab = [keep.tile([P, T2], I32, name="assay_tab%d" % a, align_bytes=64) for a in range(2)]
+        frag_tab_sc = keep.tile([P, T // 4], I32, name="frag_tab_sc", align_bytes=64)
+        assay_tab_sc = keep.tile([P, T2 // 4], I32, name="assay_tab_sc", align_bytes=64)
+        w4 = keep.tile([P, 2 * N], U8, name="w4", align_bytes=64)
+        w4_sc = keep.tile([P, N // 4], I32, name="w4_sc", align_bytes=64)
+        wn_raw = keep.tile([P, PACK, N], F32, name="wn_raw", align_bytes=64)
+        fw_sb = keep.tile([P, 2, PACK], F32, name="fw_sb")
+        base_sb = keep.tile([P, N // P], F32, name="base_sb")
+        warm = keep.tile([P, 2], F32, name="warm")
+
+        nc.scalar.dma_start(out=fw_sb[:], in_=fw.rearrange("(g p t) -> p g t", g=2, t=PACK))
+        nc.vector.memset(frag_tab_sc[:], 0)
+        nc.vector.memset(assay_tab_sc[:], 0)
+        nc.vector.memset(w4_sc[:], 0)
+        nc.vector.memset(warm[:, 0:1], 0.0)
+        nc.scalar.activation(warm[:, 1:2], warm[:, 0:1], ACT.Square, bias=1.0)
+
+        def words(tab, a):
+            return tab[a].rearrange("p t i -> p (t i)").bitcast(I32)
+
+        nc.sync.dma_start(out=assay_tab[0][:], in_=words(tab2_words, 0))
+        nc.sync.dma_start(assay_list[:], offs2)
+        nc.sync.dma_start(frag_list[:], offs)
+        nc.sync.dma_start(out=frag_tab[0][:], in_=words(tab_words, 0))
+        nc.sync.dma_start(out=frag_tab[1][:], in_=words(tab_words, 1))
+        nc.sync.dma_start(out=assay_tab[1][:], in_=words(tab2_words, 1))
+        nc.sync.dma_start(out=wn_raw[:], in_=wn.rearrange("(p t) n -> p t n", t=PACK))
+        nc.sync.dma_start(out=w4[:].bitcast(I32), in_=w4_words[0].bitcast(I32))
+        with nc.allow_non_contiguous_dma(reason="one bias value a partition"):
+            nc.sync.dma_start(out=base_sb[:], in_=base.rearrange("(c p) -> p c", p=P))
+        for q in range(4):
+            nc.sync.dma_start(out=w4_sc[32 * q : 32 * q + 4, :], in_=w4_scales[0, 4 * q : 4 * q + 4, :].bitcast(I32))
+
+        for q in range(4):
+            r = 32 * q + FRAG_ROW[0]
+            nc.gpsimd.dma_start(out=frag_tab_sc[r : r + 8, :], in_=tab_scales[:, 4 * q : 4 * q + 4, :].bitcast(I32))
+        for q in range(4):
+            r = 32 * q + ASSAY_ROW[0]
+            nc.gpsimd.dma_start(out=assay_tab_sc[r : r + 8, :], in_=tab2_scales[:, 4 * q : 4 * q + 4, :].bitcast(I32))
+
+        frag = [[keep.tile([P, KP], U32, name="frag%d%d" % (a, g), align_bytes=64) for g in range(2)] for a in range(2)]
+        assay = [[keep.tile([P, JW], U32, name="assay%d%d" % (a, h), align_bytes=64) for h in range(2)] for a in range(2)]
+        frag_sc_listed = keep.tile([P, S], U8, name="frag_sc_listed", align_bytes=64)
+        frag_sc = keep.tile([P, S], U8, name="frag_sc", align_bytes=64)
+        assay_sc = keep.tile([P, S2], U8, name="assay_sc", align_bytes=64)
+
+        def gather_frag(a, g):
+            nc.vector.tensor_copy(
+                frag[a][g][:].rearrange("p (t m) -> p m t", t=PACK),
+                frag_tab[a][:].bitcast(U32).indirect(frag_list[:, 32 * g : 32 * g + 32]),
+            )
+
+        def gather_assay(a, h):
+            nc.vector.tensor_copy(
+                assay[a][h][:], assay_tab[a][:].bitcast(U32).indirect(assay_list[:, 32 * h : 32 * h + 32])
+            )
+
+        gather_assay(0, 0)
+        gather_assay(0, 1)
+        nc.vector.tensor_copy(frag_sc_listed[:], frag_tab_sc[:].bitcast(U8).indirect(frag_list[:]))
+        nc.vector.tensor_copy(assay_sc[:], assay_tab_sc[:].bitcast(U8).indirect(assay_list[:]))
+        nc.vector.tensor_copy(
+            frag_sc[:].rearrange("p (g t m) -> p g t m", g=2, t=PACK),
+            frag_sc_listed[:].rearrange("p (g m t) -> p g t m", g=2, t=PACK),
+        )
+        gather_frag(0, 0)
+        gather_frag(0, 1)
+        gather_frag(1, 0)
+        gather_assay(1, 0)
+        gather_frag(1, 1)
+        gather_assay(1, 1)
+
+        def a_pass(bank, a, h, g, t):
+            col = KP * g + P * t
+            nc.tensor.matmul_mx(
+                out=bank[:],
+                lhsT=frag[a][g][:, P * t : P * t + P].bitcast(FP8X4),
+                lhsT_scale=frag_sc[FRAG_ROW[a] :, col : col + P],
+                rhs=assay[a][h][:].bitcast(FP8X4),
+                rhs_scale=assay_sc[ASSAY_ROW[a] :, JW * h : JW * h + JW],
+                start=(a == 0),
+                stop=(a == 1),
+            )
+
+        def new_banks():
+            return [psum.tile([P, JW], F32, name="bank") for t in range(PACK)]
+
+        def square(banks):
+            sq = ring.tile([P, PACK, JW], F32, name="sq", align_bytes=64)
+            for t in range(PACK):
+                nc.scalar.activation(sq[:, t, :], banks[t][:], ACT.Square, bias=1.0)
+            return sq
+
+        def a_unit(h, g):
+            banks = new_banks()
+            for t in range(PACK):
+                a_pass(banks[t], 0, h, g, t)
+                a_pass(banks[t], 1, h, g, t)
+            return square(banks)
+
+        def weigh(sq, g):
+            z = ring.tile([P, JW * PACK], BF16, name="z", align_bytes=64)
+            nc.vector.tensor_tensor(
+                z[:].rearrange("p (c i t) -> p c t i", i=RUN, t=PACK),
+                sq[:].rearrange("p t (c i) -> p c t i", i=RUN),
+                fw_sb[:, g, :].unsqueeze(1).unsqueeze(3).to_broadcast([P, JW // RUN, PACK, RUN]),
+                ALU.mult,
+            )
+            return z
+
+        def quantize(src, label):
+            codes = keep.tile([P, JW], U32, name=label + "_codes", align_bytes=64)
+            scales = keep.tile([P, JW], U8, name=label + "_scales", align_bytes=64)
+            nc.vector.quantize_mx(out=codes[:].bitcast(FP8X4), scales=scales[:], in_=src[:])
+            return codes, scales
+
+        def y_half(h, zq0, zq1, wq):
+            banks = new_banks()
+            for c in range(N // P):
+                nc.tensor.matmul_mx(
+                    out=banks[c][:],
+                    lhsT=w4[:, 2 * P * c : 2 * P * (c + 1)].bitcast(FP4X4),
+                    lhsT_scale=w4_sc[:].bitcast(U8)[:, P * c : P * (c + 1)],
+                    rhs=zq0[0][:].bitcast(FP8X4),
+                    rhs_scale=zq0[1][:],
+                    start=True,
+                    stop=False,
+                )
+            for c in range(N // P):
+                nc.tensor.matmul_mx(
+                    out=banks[c][:],
+                    lhsT=wq[0][:, P * c : P * (c + 1)].bitcast(FP8X4),
+                    lhsT_scale=wq[1][:, P * c : P * (c + 1)],
+                    rhs=zq1[0][:].bitcast(FP8X4),
+                    rhs_scale=zq1[1][:],
+                    start=False,
+                    stop=True,
+                )
+                res = keep.tile([P, JW], F32, name="res%d%d" % (h, c), align_bytes=64)
+                if h == 1 and c % 2 == 1:
+                    nc.vector.tensor_scalar(res[:], banks[c][:], base_sb[:, c : c + 1], None, ALU.add)
+                else:
+                    nc.scalar.activation(res[:], banks[c][:], ACT.Identity, bias=base_sb[:, c : c + 1])
+                nc.sync.dma_start(out=out[P * c : P * (c + 1), JW * h : JW * (h + 1)], in_=res[:])
+
+        first = [new_banks(), new_banks()]
+        for g in range(2):
+            for t in range(PACK):
+                a_pass(first[g][t], 0, 0, g, t)
+        sq = {}
+        for g in range(2):
+            for t in range(PACK):
+                a_pass(first[g][t], 1, 0, g, t)
+            sq[0, g] = square(first[g])
+        sq[1, 0] = a_unit(1, 0)
+
+        wn_il = keep.tile([P, N * PACK], BF16, name="wn_il", align_bytes=64)
+        nc.vector.tensor_copy(
+            wn_il[:].rearrange("p (c i t) -> p c t i", i=RUN, t=PACK),
+            wn_raw[:].rearrange("p t (c i) -> p c t i", i=RUN),
+        )
+        z00 = weigh(sq[0, 0], 0)
+        wq = quantize(wn_il, "wn")
+        zq00 = quantize(z00, "z00")
+        sq[1, 1] = a_unit(1, 1)
+        z01 = weigh(sq[0, 1], 1)
+        z10 = weigh(sq[1, 0], 0)
+        zq01 = quantize(z01, "z01")
+        y_half(0, zq00, zq01, wq)
+        z11 = weigh(sq[1, 1], 1)
+        zq10 = quantize(z10, "z10")
+        zq11 = quantize(z11, "z11")
+        y_half(1, zq10, zq11, wq)

@@ -21,6 +21,7 @@ PACK = 4
 KP = P * PACK
 JW = 512
 RUN = 4
+WN_SPLIT = 64
 FRAG_ROW = (0, 4)
 ASSAY_ROW = (8, 12)
 
@@ -31,7 +32,7 @@ def tile_list_fragment_assay_screen_kernel(
     nc = tc.nc
     with ExitStack() as ctx:
         keep = ctx.enter_context(tc.tile_pool(name="keep", bufs=1))
-        ring = ctx.enter_context(tc.tile_pool(name="ring", bufs=3))
+        ring = ctx.enter_context(tc.tile_pool(name="ring", bufs=4))
         psum = ctx.enter_context(tc.psum_pool(name="psum", bufs=8))
 
         frag_list = keep.tile([P, S // 16], U16, name="frag_list")
@@ -47,7 +48,6 @@ def tile_list_fragment_assay_screen_kernel(
         base_sb = keep.tile([P, N // P], F32, name="base_sb")
         warm = keep.tile([P, 2], F32, name="warm")
 
-        nc.scalar.dma_start(out=fw_sb[:], in_=fw.rearrange("(g p t) -> p g t", g=2, t=PACK))
         nc.vector.memset(frag_tab_sc[:], 0)
         nc.vector.memset(assay_tab_sc[:], 0)
         nc.vector.memset(w4_sc[:], 0)
@@ -57,25 +57,25 @@ def tile_list_fragment_assay_screen_kernel(
         def words(tab, a):
             return tab[a].rearrange("p t i -> p (t i)").bitcast(I32)
 
-        nc.sync.dma_start(out=assay_tab[0][:], in_=words(tab2_words, 0))
         nc.sync.dma_start(assay_list[:], offs2)
         nc.sync.dma_start(frag_list[:], offs)
+        nc.sync.dma_start(out=assay_tab[0][:], in_=words(tab2_words, 0))
+        for q in range(4):
+            r = 32 * q + FRAG_ROW[0]
+            nc.sync.dma_start(out=frag_tab_sc[r : r + 8, :], in_=tab_scales[:, 4 * q : 4 * q + 4, :].bitcast(I32))
         nc.sync.dma_start(out=frag_tab[0][:], in_=words(tab_words, 0))
+        for q in range(4):
+            r = 32 * q + ASSAY_ROW[0]
+            nc.sync.dma_start(out=assay_tab_sc[r : r + 8, :], in_=tab2_scales[:, 4 * q : 4 * q + 4, :].bitcast(I32))
         nc.sync.dma_start(out=frag_tab[1][:], in_=words(tab_words, 1))
         nc.sync.dma_start(out=assay_tab[1][:], in_=words(tab2_words, 1))
+        nc.sync.dma_start(out=fw_sb[:], in_=fw.rearrange("(g p t) -> p g t", g=2, t=PACK))
         nc.sync.dma_start(out=wn_raw[:], in_=wn.rearrange("(p t) n -> p t n", t=PACK))
         nc.sync.dma_start(out=w4[:].bitcast(I32), in_=w4_words[0].bitcast(I32))
         with nc.allow_non_contiguous_dma(reason="one bias value a partition"):
             nc.sync.dma_start(out=base_sb[:], in_=base.rearrange("(c p) -> p c", p=P))
         for q in range(4):
             nc.sync.dma_start(out=w4_sc[32 * q : 32 * q + 4, :], in_=w4_scales[0, 4 * q : 4 * q + 4, :].bitcast(I32))
-
-        for q in range(4):
-            r = 32 * q + FRAG_ROW[0]
-            nc.gpsimd.dma_start(out=frag_tab_sc[r : r + 8, :], in_=tab_scales[:, 4 * q : 4 * q + 4, :].bitcast(I32))
-        for q in range(4):
-            r = 32 * q + ASSAY_ROW[0]
-            nc.gpsimd.dma_start(out=assay_tab_sc[r : r + 8, :], in_=tab2_scales[:, 4 * q : 4 * q + 4, :].bitcast(I32))
 
         frag = [[keep.tile([P, KP], U32, name="frag%d%d" % (a, g), align_bytes=64) for g in range(2)] for a in range(2)]
         assay = [[keep.tile([P, JW], U32, name="assay%d%d" % (a, h), align_bytes=64) for h in range(2)] for a in range(2)]
@@ -97,13 +97,13 @@ def tile_list_fragment_assay_screen_kernel(
         gather_assay(0, 0)
         gather_assay(0, 1)
         nc.vector.tensor_copy(frag_sc_listed[:], frag_tab_sc[:].bitcast(U8).indirect(frag_list[:]))
-        nc.vector.tensor_copy(assay_sc[:], assay_tab_sc[:].bitcast(U8).indirect(assay_list[:]))
         nc.vector.tensor_copy(
             frag_sc[:].rearrange("p (g t m) -> p g t m", g=2, t=PACK),
             frag_sc_listed[:].rearrange("p (g m t) -> p g t m", g=2, t=PACK),
         )
         gather_frag(0, 0)
         gather_frag(0, 1)
+        nc.vector.tensor_copy(assay_sc[:], assay_tab_sc[:].bitcast(U8).indirect(assay_list[:]))
         gather_frag(1, 0)
         gather_assay(1, 0)
         gather_frag(1, 1)
@@ -194,17 +194,17 @@ def tile_list_fragment_assay_screen_kernel(
         sq[1, 0] = a_unit(1, 0)
 
         wn_il = keep.tile([P, N * PACK], BF16, name="wn_il", align_bytes=64)
-        nc.vector.tensor_copy(
-            wn_il[:].rearrange("p (c i t) -> p c t i", i=RUN, t=PACK),
-            wn_raw[:].rearrange("p t (c i) -> p c t i", i=RUN),
-        )
+        wn_dst = wn_il[:].rearrange("p (c i t) -> p c t i", i=RUN, t=PACK)
+        wn_src = wn_raw[:].rearrange("p t (c i) -> p c t i", i=RUN)
+        nc.vector.tensor_copy(wn_dst[:, :WN_SPLIT], wn_src[:, :WN_SPLIT])
+        nc.scalar.copy(wn_dst[:, WN_SPLIT:], wn_src[:, WN_SPLIT:])
         z00 = weigh(sq[0, 0], 0)
-        wq = quantize(wn_il, "wn")
-        zq00 = quantize(z00, "z00")
         sq[1, 1] = a_unit(1, 1)
         z01 = weigh(sq[0, 1], 1)
+        zq00 = quantize(z00, "z00")
         z10 = weigh(sq[1, 0], 0)
         zq01 = quantize(z01, "z01")
+        wq = quantize(wn_il, "wn")
         y_half(0, zq00, zq01, wq)
         z11 = weigh(sq[1, 1], 1)
         zq10 = quantize(z10, "z10")

@@ -21,6 +21,7 @@ PACK = 4
 KP = P * PACK
 JW = 512
 RUN = 4
+CW = 256
 WN_SPLIT = 64
 FRAG_ROW = (0, 4)
 ASSAY_ROW = (8, 12)
@@ -32,7 +33,7 @@ def tile_list_fragment_assay_screen_kernel(
     nc = tc.nc
     with ExitStack() as ctx:
         keep = ctx.enter_context(tc.tile_pool(name="keep", bufs=1))
-        ring = ctx.enter_context(tc.tile_pool(name="ring", bufs=4))
+        ring = ctx.enter_context(tc.tile_pool(name="ring", bufs=5))
         psum = ctx.enter_context(tc.psum_pool(name="psum", bufs=8))
 
         frag_list = keep.tile([P, S // 16], U16, name="frag_list")
@@ -105,47 +106,63 @@ def tile_list_fragment_assay_screen_kernel(
         gather_frag(0, 1)
         nc.vector.tensor_copy(assay_sc[:], assay_tab_sc[:].bitcast(U8).indirect(assay_list[:]))
         gather_frag(1, 0)
-        gather_assay(1, 0)
         gather_frag(1, 1)
+        for c in range(2):
+            nc.vector.tensor_copy(
+                assay[1][0][:, CW * c : CW * (c + 1)],
+                assay_tab[1][:].bitcast(U32).indirect(assay_list[:, 16 * c : 16 * c + 16]),
+            )
         gather_assay(1, 1)
 
-        def a_pass(bank, a, h, g, t):
+        def a_pass(bank, a, c, g, t):
             col = KP * g + P * t
             nc.tensor.matmul_mx(
-                out=bank[:],
+                out=bank[:, t % 2, :],
                 lhsT=frag[a][g][:, P * t : P * t + P].bitcast(FP8X4),
                 lhsT_scale=frag_sc[FRAG_ROW[a] :, col : col + P],
-                rhs=assay[a][h][:].bitcast(FP8X4),
-                rhs_scale=assay_sc[ASSAY_ROW[a] :, JW * h : JW * h + JW],
+                rhs=assay[a][c // 2][:, CW * (c % 2) : CW * (c % 2 + 1)].bitcast(FP8X4),
+                rhs_scale=assay_sc[ASSAY_ROW[a] :, CW * c : CW * (c + 1)],
                 start=(a == 0),
                 stop=(a == 1),
             )
 
-        def new_banks():
-            return [psum.tile([P, JW], F32, name="bank") for t in range(PACK)]
+        def a_open(c, g):
+            banks = [psum.tile([P, 2, CW], F32, name="bank") for u in range(2)]
+            for u in range(2):
+                a_pass(banks[u], 0, c, g, 2 * u)
+            return banks
 
-        def square(banks):
-            sq = ring.tile([P, PACK, JW], F32, name="sq", align_bytes=64)
-            for t in range(PACK):
-                nc.scalar.activation(sq[:, t, :], banks[t][:], ACT.Square, bias=1.0)
+        def a_close(banks, c, g):
+            sq = ring.tile([P, 2, CW, 2], F32, name="sq", align_bytes=64)
+            for u in range(2):
+                a_pass(banks[u], 1, c, g, 2 * u)
+                a_pass(banks[u], 0, c, g, 2 * u + 1)
+                a_pass(banks[u], 1, c, g, 2 * u + 1)
+                nc.scalar.activation(sq[:, u], banks[u][:].rearrange("p e n -> p n e"), ACT.Square, bias=1.0)
             return sq
 
-        def a_unit(h, g):
-            banks = new_banks()
-            for t in range(PACK):
-                a_pass(banks[t], 0, h, g, t)
-                a_pass(banks[t], 1, h, g, t)
-            return square(banks)
-
         def weigh(sq, g):
-            z = ring.tile([P, JW * PACK], BF16, name="z", align_bytes=64)
+            z = ring.tile([P, CW * PACK], BF16, name="z", align_bytes=64)
             nc.vector.tensor_tensor(
-                z[:].rearrange("p (c i t) -> p c t i", i=RUN, t=PACK),
-                sq[:].rearrange("p t (c i) -> p c t i", i=RUN),
-                fw_sb[:, g, :].unsqueeze(1).unsqueeze(3).to_broadcast([P, JW // RUN, PACK, RUN]),
+                z[:].rearrange("p (n u e) -> p n u e", u=2, e=2),
+                sq[:].rearrange("p u n e -> p n u e"),
+                fw_sb[:, g, :].rearrange("p (u e) -> p u e", u=2).unsqueeze(1).to_broadcast([P, CW, 2, 2]),
                 ALU.mult,
             )
             return z
+
+        zq = {}
+        for h in range(2):
+            for g in range(2):
+                zq[h, g] = (
+                    keep.tile([P, JW], U32, name="z_codes%d%d" % (h, g), align_bytes=64),
+                    keep.tile([P, JW], U8, name="z_scales%d%d" % (h, g), align_bytes=64),
+                )
+
+        def quantize_z(z, c, g):
+            codes, scales = zq[c // 2, g]
+            cols = slice(CW * (c % 2), CW * (c % 2 + 1))
+            nc.vector.quantize_mx(out=codes[:, cols].bitcast(FP8X4), scales=scales[:, cols], in_=z[:])
 
         def quantize(src, label):
             codes = keep.tile([P, JW], U32, name=label + "_codes", align_bytes=64)
@@ -153,60 +170,61 @@ def tile_list_fragment_assay_screen_kernel(
             nc.vector.quantize_mx(out=codes[:].bitcast(FP8X4), scales=scales[:], in_=src[:])
             return codes, scales
 
-        def y_half(h, zq0, zq1, wq):
-            banks = new_banks()
-            for c in range(N // P):
-                nc.tensor.matmul_mx(
-                    out=banks[c][:],
-                    lhsT=w4[:, 2 * P * c : 2 * P * (c + 1)].bitcast(FP4X4),
-                    lhsT_scale=w4_sc[:].bitcast(U8)[:, P * c : P * (c + 1)],
-                    rhs=zq0[0][:].bitcast(FP8X4),
-                    rhs_scale=zq0[1][:],
-                    start=True,
-                    stop=False,
-                )
-            for c in range(N // P):
-                nc.tensor.matmul_mx(
-                    out=banks[c][:],
-                    lhsT=wq[0][:, P * c : P * (c + 1)].bitcast(FP8X4),
-                    lhsT_scale=wq[1][:, P * c : P * (c + 1)],
-                    rhs=zq1[0][:].bitcast(FP8X4),
-                    rhs_scale=zq1[1][:],
-                    start=False,
-                    stop=True,
-                )
-                res = keep.tile([P, JW], F32, name="res%d%d" % (h, c), align_bytes=64)
-                if h == 1 and c % 2 == 1:
-                    nc.vector.tensor_scalar(res[:], banks[c][:], base_sb[:, c : c + 1], None, ALU.add)
+        def y_pass(dst, g, r, h, cols, wq):
+            if g == 0:
+                lhsT = w4[:, 2 * P * r : 2 * P * (r + 1)].bitcast(FP4X4)
+                lhsT_scale = w4_sc[:].bitcast(U8)[:, P * r : P * (r + 1)]
+            else:
+                lhsT = wq[0][:, P * r : P * (r + 1)].bitcast(FP8X4)
+                lhsT_scale = wq[1][:, P * r : P * (r + 1)]
+            nc.tensor.matmul_mx(
+                out=dst,
+                lhsT=lhsT,
+                lhsT_scale=lhsT_scale,
+                rhs=zq[h, g][0][:, cols].bitcast(FP8X4),
+                rhs_scale=zq[h, g][1][:, cols],
+                start=(g == 0),
+                stop=(g == 1),
+            )
+
+        def y_block(j0, width, group, wq, on_vector):
+            h, off = divmod(j0, JW)
+            banks = [psum.tile([P, width], F32, name="bank") for r in range(N // P)]
+            for r in range(N // P):
+                y_pass(banks[r][:, :group], 0, r, h, slice(off, off + group), wq)
+            for r in range(N // P):
+                y_pass(banks[r][:, :group], 1, r, h, slice(off, off + group), wq)
+                for s in range(group, width, group):
+                    for g in range(2):
+                        y_pass(banks[r][:, s : s + group], g, r, h, slice(off + s, off + s + group), wq)
+                res = keep.tile([P, width], F32, name="res%d_%d" % (j0, r), align_bytes=64)
+                if r in on_vector:
+                    nc.vector.tensor_scalar(res[:], banks[r][:], base_sb[:, r : r + 1], None, ALU.add)
                 else:
-                    nc.scalar.activation(res[:], banks[c][:], ACT.Identity, bias=base_sb[:, c : c + 1])
-                nc.sync.dma_start(out=out[P * c : P * (c + 1), JW * h : JW * (h + 1)], in_=res[:])
+                    nc.scalar.activation(res[:], banks[r][:], ACT.Identity, bias=base_sb[:, r : r + 1])
+                nc.sync.dma_start(out=out[P * r : P * (r + 1), j0 : j0 + width], in_=res[:])
 
-        first = [new_banks(), new_banks()]
-        for g in range(2):
-            for t in range(PACK):
-                a_pass(first[g][t], 0, 0, g, t)
-        sq = {}
-        for g in range(2):
-            for t in range(PACK):
-                a_pass(first[g][t], 1, 0, g, t)
-            sq[0, g] = square(first[g])
-        sq[1, 0] = a_unit(1, 0)
-
+        units = [(0, 0), (1, 0), (0, 1), (1, 1), (2, 0), (2, 1), (3, 0), (3, 1)]
+        opened = [a_open(c, g) for c, g in units[:4]]
+        sq = [a_close(opened[k], *units[k]) for k in range(4)]
         wn_il = keep.tile([P, N * PACK], BF16, name="wn_il", align_bytes=64)
         wn_dst = wn_il[:].rearrange("p (c i t) -> p c t i", i=RUN, t=PACK)
         wn_src = wn_raw[:].rearrange("p t (c i) -> p c t i", i=RUN)
-        nc.vector.tensor_copy(wn_dst[:, :WN_SPLIT], wn_src[:, :WN_SPLIT])
-        nc.scalar.copy(wn_dst[:, WN_SPLIT:], wn_src[:, WN_SPLIT:])
-        z00 = weigh(sq[0, 0], 0)
-        sq[1, 1] = a_unit(1, 1)
-        z01 = weigh(sq[0, 1], 1)
-        zq00 = quantize(z00, "z00")
-        z10 = weigh(sq[1, 0], 0)
-        zq01 = quantize(z01, "z01")
-        wq = quantize(wn_il, "wn")
-        y_half(0, zq00, zq01, wq)
-        z11 = weigh(sq[1, 1], 1)
-        zq10 = quantize(z10, "z10")
-        zq11 = quantize(z11, "z11")
-        y_half(1, zq10, zq11, wq)
+        z = []
+        for k in range(8):
+            z.append(weigh(sq[k], units[k][1]))
+            if k < 4:
+                sq.append(a_close(a_open(*units[k + 4]), *units[k + 4]))
+            if k == 0:
+                nc.vector.tensor_copy(wn_dst[:, :WN_SPLIT], wn_src[:, :WN_SPLIT])
+            if k == 1:
+                nc.scalar.copy(wn_dst[:, WN_SPLIT:], wn_src[:, WN_SPLIT:])
+            if k > 0:
+                quantize_z(z[k - 1], *units[k - 1])
+            if k == 4:
+                wq = quantize(wn_il, "wn")
+                y_block(0, JW, JW, wq, ())
+            if k == 6:
+                y_block(2 * CW, CW, P, wq, ())
+        quantize_z(z[7], *units[7])
+        y_block(3 * CW, CW, P, wq, (1, 3))

@@ -24,7 +24,7 @@ RUN = 4
 CW = 256
 WN_SPLIT = 64
 FRAG_ROW = (0, 4)
-ASSAY_ROW = (8, 12)
+ASSAY_ROW = (0, 4)
 
 
 def tile_list_fragment_assay_screen_kernel(
@@ -84,10 +84,17 @@ def tile_list_fragment_assay_screen_kernel(
         frag_sc = keep.tile([P, S], U8, name="frag_sc", align_bytes=64)
         assay_sc = keep.tile([P, S2], U8, name="assay_sc", align_bytes=64)
 
+        listed = [[keep.tile([P, KP], U32, name="listed%d%d" % (a, g), align_bytes=64) for g in range(2)] for a in range(2)]
+
         def gather_frag(a, g):
             nc.vector.tensor_copy(
-                frag[a][g][:].rearrange("p (t m) -> p m t", t=PACK),
-                frag_tab[a][:].bitcast(U32).indirect(frag_list[:, 32 * g : 32 * g + 32]),
+                listed[a][g][:], frag_tab[a][:].bitcast(U32).indirect(frag_list[:, 32 * g : 32 * g + 32])
+            )
+
+        def sort_frag(a, g):
+            nc.vector.tensor_copy(
+                frag[a][g][:].bitcast(I32).rearrange("p (t c i) -> p c t i", t=PACK, i=RUN),
+                listed[a][g][:].bitcast(I32).rearrange("p (c i t) -> p c t i", t=PACK, i=RUN),
             )
 
         def gather_assay(a, h):
@@ -104,10 +111,13 @@ def tile_list_fragment_assay_screen_kernel(
         )
         gather_frag(0, 0)
         gather_frag(0, 1)
+        sort_frag(0, 0)
         nc.vector.tensor_copy(assay_sc[:], assay_tab_sc[:].bitcast(U8).indirect(assay_list[:]))
+        sort_frag(0, 1)
         gather_frag(1, 0)
         gather_frag(1, 1)
         for c in range(2):
+            sort_frag(1, c)
             nc.vector.tensor_copy(
                 assay[1][0][:, CW * c : CW * (c + 1)],
                 assay_tab[1][:].bitcast(U32).indirect(assay_list[:, 16 * c : 16 * c + 16]),

@@ -49,8 +49,8 @@ def tile_list_fragment_assay_screen_kernel(
         base_sb = keep.tile([P, N // P], F32, name="base_sb")
         warm = keep.tile([P, 2], F32, name="warm")
 
-        nc.vector.memset(frag_tab_sc[:], 0)
         nc.vector.memset(assay_tab_sc[:], 0)
+        nc.vector.memset(frag_tab_sc[:], 0)
         nc.vector.memset(w4_sc[:], 0)
         nc.vector.memset(warm[:, 0:1], 0.0)
         nc.scalar.activation(warm[:, 1:2], warm[:, 0:1], ACT.Square, bias=1.0)
@@ -61,13 +61,12 @@ def tile_list_fragment_assay_screen_kernel(
         nc.sync.dma_start(assay_list[:], offs2)
         nc.sync.dma_start(frag_list[:], offs)
         nc.sync.dma_start(out=assay_tab[0][:], in_=words(tab2_words, 0))
-        for q in range(4):
-            r = 32 * q + FRAG_ROW[0]
-            nc.sync.dma_start(out=frag_tab_sc[r : r + 8, :], in_=tab_scales[:, 4 * q : 4 * q + 4, :].bitcast(I32))
+        for plane, rows in ((assay_tab_sc, tab2_scales), (frag_tab_sc, tab_scales)):
+            for q in (2, 0, 3, 1):
+                nc.sync.dma_start(out=plane[32 * q : 32 * q + 8, :], in_=rows[:, 4 * q : 4 * q + 4, :].bitcast(I32))
+        for r in range(4):
+            nc.sync.dma_start(out=w4_sc[r:P:32, :], in_=w4_scales[0, r:16:4, :].bitcast(I32))
         nc.sync.dma_start(out=frag_tab[0][:], in_=words(tab_words, 0))
-        for q in range(4):
-            r = 32 * q + ASSAY_ROW[0]
-            nc.sync.dma_start(out=assay_tab_sc[r : r + 8, :], in_=tab2_scales[:, 4 * q : 4 * q + 4, :].bitcast(I32))
         nc.sync.dma_start(out=frag_tab[1][:], in_=words(tab_words, 1))
         nc.sync.dma_start(out=assay_tab[1][:], in_=words(tab2_words, 1))
         nc.sync.dma_start(out=fw_sb[:], in_=fw.rearrange("(g p t) -> p g t", g=2, t=PACK))
@@ -75,8 +74,6 @@ def tile_list_fragment_assay_screen_kernel(
         nc.sync.dma_start(out=w4[:].bitcast(I32), in_=w4_words[0].bitcast(I32))
         with nc.allow_non_contiguous_dma(reason="one bias value a partition"):
             nc.sync.dma_start(out=base_sb[:], in_=base.rearrange("(c p) -> p c", p=P))
-        for q in range(4):
-            nc.sync.dma_start(out=w4_sc[32 * q : 32 * q + 4, :], in_=w4_scales[0, 4 * q : 4 * q + 4, :].bitcast(I32))
 
         frag = [[keep.tile([P, KP], U32, name="frag%d%d" % (a, g), align_bytes=64) for g in range(2)] for a in range(2)]
         assay = [[keep.tile([P, JW], U32, name="assay%d%d" % (a, h), align_bytes=64) for h in range(2)] for a in range(2)]
@@ -84,17 +81,10 @@ def tile_list_fragment_assay_screen_kernel(
         frag_sc = keep.tile([P, S], U8, name="frag_sc", align_bytes=64)
         assay_sc = keep.tile([P, S2], U8, name="assay_sc", align_bytes=64)
 
-        listed = [[keep.tile([P, KP], U32, name="listed%d%d" % (a, g), align_bytes=64) for g in range(2)] for a in range(2)]
-
         def gather_frag(a, g):
             nc.vector.tensor_copy(
-                listed[a][g][:], frag_tab[a][:].bitcast(U32).indirect(frag_list[:, 32 * g : 32 * g + 32])
-            )
-
-        def sort_frag(a, g):
-            nc.vector.tensor_copy(
-                frag[a][g][:].bitcast(I32).rearrange("p (t c i) -> p c t i", t=PACK, i=RUN),
-                listed[a][g][:].bitcast(I32).rearrange("p (c i t) -> p c t i", t=PACK, i=RUN),
+                frag[a][g][:].rearrange("p (t m) -> p m t", t=PACK),
+                frag_tab[a][:].bitcast(U32).indirect(frag_list[:, 32 * g : 32 * g + 32]),
             )
 
         def gather_assay(a, h):
@@ -102,8 +92,15 @@ def tile_list_fragment_assay_screen_kernel(
                 assay[a][h][:], assay_tab[a][:].bitcast(U32).indirect(assay_list[:, 32 * h : 32 * h + 32])
             )
 
+        def gather_assay_chunk(c):
+            nc.vector.tensor_copy(
+                assay[1][0][:, CW * c : CW * (c + 1)],
+                assay_tab[1][:].bitcast(U32).indirect(assay_list[:, 16 * c : 16 * c + 16]),
+            )
+
         gather_assay(0, 0)
         gather_assay(0, 1)
+        nc.vector.tensor_copy(assay_sc[:], assay_tab_sc[:].bitcast(U8).indirect(assay_list[:]))
         nc.vector.tensor_copy(frag_sc_listed[:], frag_tab_sc[:].bitcast(U8).indirect(frag_list[:]))
         nc.vector.tensor_copy(
             frag_sc[:].rearrange("p (g t m) -> p g t m", g=2, t=PACK),
@@ -111,17 +108,10 @@ def tile_list_fragment_assay_screen_kernel(
         )
         gather_frag(0, 0)
         gather_frag(0, 1)
-        sort_frag(0, 0)
-        nc.vector.tensor_copy(assay_sc[:], assay_tab_sc[:].bitcast(U8).indirect(assay_list[:]))
-        sort_frag(0, 1)
         gather_frag(1, 0)
         gather_frag(1, 1)
-        for c in range(2):
-            sort_frag(1, c)
-            nc.vector.tensor_copy(
-                assay[1][0][:, CW * c : CW * (c + 1)],
-                assay_tab[1][:].bitcast(U32).indirect(assay_list[:, 16 * c : 16 * c + 16]),
-            )
+        gather_assay_chunk(0)
+        gather_assay_chunk(1)
         gather_assay(1, 1)
 
         def a_pass(bank, a, c, g, t):
@@ -151,12 +141,12 @@ def tile_list_fragment_assay_screen_kernel(
                 nc.scalar.activation(sq[:, u], banks[u][:].rearrange("p e n -> p n e"), ACT.Square, bias=1.0)
             return sq
 
-        def weigh(sq, g):
-            z = ring.tile([P, CW * PACK], BF16, name="z", align_bytes=64)
+        def weigh(sq, g, lo, width):
+            z = ring.tile([P, width * PACK], BF16, name="z", align_bytes=64)
             nc.vector.tensor_tensor(
                 z[:].rearrange("p (n u e) -> p n u e", u=2, e=2),
-                sq[:].rearrange("p u n e -> p n u e"),
-                fw_sb[:, g, :].rearrange("p (u e) -> p u e", u=2).unsqueeze(1).to_broadcast([P, CW, 2, 2]),
+                sq[:, :, lo : lo + width, :].rearrange("p u n e -> p n u e"),
+                fw_sb[:, g, :].rearrange("p (u e) -> p u e", u=2).unsqueeze(1).to_broadcast([P, width, 2, 2]),
                 ALU.mult,
             )
             return z
@@ -169,9 +159,9 @@ def tile_list_fragment_assay_screen_kernel(
                     keep.tile([P, JW], U8, name="z_scales%d%d" % (h, g), align_bytes=64),
                 )
 
-        def quantize_z(z, c, g):
+        def quantize_z(z, c, g, lo, width):
             codes, scales = zq[c // 2, g]
-            cols = slice(CW * (c % 2), CW * (c % 2 + 1))
+            cols = slice(CW * (c % 2) + lo, CW * (c % 2) + lo + width)
             nc.vector.quantize_mx(out=codes[:, cols].bitcast(FP8X4), scales=scales[:, cols], in_=z[:])
 
         def quantize(src, label):
@@ -197,9 +187,12 @@ def tile_list_fragment_assay_screen_kernel(
                 stop=(g == 1),
             )
 
-        def y_block(j0, width, group, wq, on_vector):
+        out_tiles = out.rearrange("(r p) j -> p r j", p=P)
+
+        def y_block(j0, width, group, wq, on_vector, per_store):
             h, off = divmod(j0, JW)
             banks = [psum.tile([P, width], F32, name="bank") for r in range(N // P)]
+            res = keep.tile([P, N // P, width], F32, name="res%d" % j0, align_bytes=64)
             for r in range(N // P):
                 y_pass(banks[r][:, :group], 0, r, h, slice(off, off + group), wq)
             for r in range(N // P):
@@ -207,12 +200,13 @@ def tile_list_fragment_assay_screen_kernel(
                 for s in range(group, width, group):
                     for g in range(2):
                         y_pass(banks[r][:, s : s + group], g, r, h, slice(off + s, off + s + group), wq)
-                res = keep.tile([P, width], F32, name="res%d_%d" % (j0, r), align_bytes=64)
                 if r in on_vector:
-                    nc.vector.tensor_scalar(res[:], banks[r][:], base_sb[:, r : r + 1], None, ALU.add)
+                    nc.vector.tensor_scalar(res[:, r, :], banks[r][:], base_sb[:, r : r + 1], None, ALU.add)
                 else:
-                    nc.scalar.activation(res[:], banks[r][:], ACT.Identity, bias=base_sb[:, r : r + 1])
-                nc.sync.dma_start(out=out[P * r : P * (r + 1), j0 : j0 + width], in_=res[:])
+                    nc.scalar.activation(res[:, r, :], banks[r][:], ACT.Identity, bias=base_sb[:, r : r + 1])
+                if (r + 1) % per_store == 0:
+                    rows = slice(r + 1 - per_store, r + 1)
+                    nc.sync.dma_start(out=out_tiles[:, rows, j0 : j0 + width], in_=res[:, rows, :])
 
         units = [(0, 0), (1, 0), (0, 1), (1, 1), (2, 0), (2, 1), (3, 0), (3, 1)]
         opened = [a_open(c, g) for c, g in units[:4]]
@@ -221,20 +215,28 @@ def tile_list_fragment_assay_screen_kernel(
         wn_dst = wn_il[:].rearrange("p (c i t) -> p c t i", i=RUN, t=PACK)
         wn_src = wn_raw[:].rearrange("p t (c i) -> p c t i", i=RUN)
         z = []
-        for k in range(8):
-            z.append(weigh(sq[k], units[k][1]))
+        for k in range(7):
+            z.append(weigh(sq[k], units[k][1], 0, CW))
             if k < 4:
                 sq.append(a_close(a_open(*units[k + 4]), *units[k + 4]))
             if k == 0:
                 nc.vector.tensor_copy(wn_dst[:, :WN_SPLIT], wn_src[:, :WN_SPLIT])
             if k == 1:
-                nc.scalar.copy(wn_dst[:, WN_SPLIT:], wn_src[:, WN_SPLIT:])
+                nc.scalar.copy(
+                    wn_il[:].rearrange("p (n t) -> p n t", t=PACK)[:, RUN * WN_SPLIT :],
+                    wn_raw[:].rearrange("p t n -> p n t")[:, RUN * WN_SPLIT :],
+                )
             if k > 0:
-                quantize_z(z[k - 1], *units[k - 1])
+                quantize_z(z[k - 1], *units[k - 1], 0, CW)
             if k == 4:
                 wq = quantize(wn_il, "wn")
-                y_block(0, JW, JW, wq, ())
+                y_block(0, JW, JW, wq, (), 1)
             if k == 6:
-                y_block(2 * CW, CW, P, wq, ())
-        quantize_z(z[7], *units[7])
-        y_block(3 * CW, CW, P, wq, (1, 3))
+                y_block(2 * CW, CW, P, wq, (), 2)
+        za = weigh(sq[7], 1, 0, P)
+        quantize_z(z[6], 3, 0, 0, CW)
+        zb = weigh(sq[7], 1, P, P)
+        quantize_z(za, 3, 1, 0, P)
+        quantize_z(zb, 3, 1, P, P)
+        y_block(3 * CW, P, P, wq, (), 4)
+        y_block(3 * CW + P, P, P, wq, (1, 3), 2)

@@ -23,8 +23,8 @@ JW = 512
 RUN = 4
 CW = 256
 WN_SPLIT = 64
-FRAG_ROW = (0, 4)
-ASSAY_ROW = (0, 4)
+PLANE_ROW = (0, 12)
+LOAD_ROW = (84, 12)
 
 
 def tile_list_fragment_assay_screen_kernel(
@@ -39,47 +39,57 @@ def tile_list_fragment_assay_screen_kernel(
         frag_list = keep.tile([P, S // 16], U16, name="frag_list")
         assay_list = keep.tile([P, S2 // 16], U16, name="assay_list")
         frag_tab = [keep.tile([P, T], I32, name="frag_tab%d" % a, align_bytes=64) for a in range(2)]
-        assay_tab = [keep.tile([P, T2], I32, name="assay_tab%d" % a, align_bytes=64) for a in range(2)]
+        assay_tab = [keep.tile([P, T2], I32, name="assay_tab0", align_bytes=64)]
         frag_tab_sc = keep.tile([P, T // 4], I32, name="frag_tab_sc", align_bytes=64)
         assay_tab_sc = keep.tile([P, T2 // 4], I32, name="assay_tab_sc", align_bytes=64)
-        w4 = keep.tile([P, 2 * N], U8, name="w4", align_bytes=64)
-        w4_sc = keep.tile([P, N // 4], I32, name="w4_sc", align_bytes=64)
-        wn_raw = keep.tile([P, PACK, N], F32, name="wn_raw", align_bytes=64)
         fw_sb = keep.tile([P, 2, PACK], F32, name="fw_sb")
-        base_sb = keep.tile([P, N // P], F32, name="base_sb")
         warm = keep.tile([P, 2], F32, name="warm")
 
-        nc.vector.memset(assay_tab_sc[:], 0)
         nc.vector.memset(frag_tab_sc[:], 0)
-        nc.vector.memset(w4_sc[:], 0)
+        nc.vector.memset(assay_tab_sc[:], 0)
         nc.vector.memset(warm[:, 0:1], 0.0)
         nc.scalar.activation(warm[:, 1:2], warm[:, 0:1], ACT.Square, bias=1.0)
 
         def words(tab, a):
             return tab[a].rearrange("p t i -> p (t i)").bitcast(I32)
 
+        half = T2 // 2
         nc.sync.dma_start(assay_list[:], offs2)
         nc.sync.dma_start(frag_list[:], offs)
-        nc.sync.dma_start(out=assay_tab[0][:], in_=words(tab2_words, 0))
-        for plane, rows in ((assay_tab_sc, tab2_scales), (frag_tab_sc, tab_scales)):
-            for q in (2, 0, 3, 1):
-                nc.sync.dma_start(out=plane[32 * q : 32 * q + 8, :], in_=rows[:, 4 * q : 4 * q + 4, :].bitcast(I32))
-        for r in range(4):
-            nc.sync.dma_start(out=w4_sc[r:P:32, :], in_=w4_scales[0, r:16:4, :].bitcast(I32))
+        nc.sync.dma_start(out=assay_tab[0][:, :half], in_=words(tab2_words, 0)[:, :half])
+        for window, rows in ((frag_tab_sc, tab_scales), (assay_tab_sc, tab2_scales)):
+            for a in range(2):
+                nc.sync.dma_start(out=window[LOAD_ROW[a] : LOAD_ROW[a] + 16, :], in_=rows[a].bitcast(I32))
+        nc.sync.dma_start(out=assay_tab[0][:, half:], in_=words(tab2_words, 0)[:, half:])
         nc.sync.dma_start(out=frag_tab[0][:], in_=words(tab_words, 0))
-        nc.sync.dma_start(out=frag_tab[1][:], in_=words(tab_words, 1))
-        nc.sync.dma_start(out=assay_tab[1][:], in_=words(tab2_words, 1))
         nc.sync.dma_start(out=fw_sb[:], in_=fw.rearrange("(g p t) -> p g t", g=2, t=PACK))
-        nc.sync.dma_start(out=wn_raw[:], in_=wn.rearrange("(p t) n -> p t n", t=PACK))
-        nc.sync.dma_start(out=w4[:].bitcast(I32), in_=w4_words[0].bitcast(I32))
-        with nc.allow_non_contiguous_dma(reason="one bias value a partition"):
-            nc.sync.dma_start(out=base_sb[:], in_=base.rearrange("(c p) -> p c", p=P))
+        nc.sync.dma_start(out=frag_tab[1][:], in_=words(tab_words, 1))
 
         frag = [[keep.tile([P, KP], U32, name="frag%d%d" % (a, g), align_bytes=64) for g in range(2)] for a in range(2)]
-        assay = [[keep.tile([P, JW], U32, name="assay%d%d" % (a, h), align_bytes=64) for h in range(2)] for a in range(2)]
+        assay = [keep.tile([P, S2], U32, name="assay%d" % a, align_bytes=64) for a in range(2)]
         frag_sc_listed = keep.tile([P, S], U8, name="frag_sc_listed", align_bytes=64)
-        frag_sc = keep.tile([P, S], U8, name="frag_sc", align_bytes=64)
-        assay_sc = keep.tile([P, S2], U8, name="assay_sc", align_bytes=64)
+        assay_sc_listed = keep.tile([P, S2], U8, name="assay_sc_listed", align_bytes=64)
+        planes = keep.tile([P, S + S2], U8, name="planes", align_bytes=64)
+
+        nc.vector.tensor_copy(frag_sc_listed[:], frag_tab_sc[:].bitcast(U8).indirect(frag_list[:]))
+        nc.vector.tensor_copy(assay_sc_listed[:], assay_tab_sc[:].bitcast(U8).indirect(assay_list[:]))
+        nc.vector.tensor_copy(
+            planes[:, :S].rearrange("p (g t m) -> p g t m", g=2, t=PACK),
+            frag_sc_listed[:].rearrange("p (g m t) -> p g t m", g=2, t=PACK),
+        )
+        nc.vector.tensor_copy(planes[:, S:].bitcast(I32), assay_sc_listed[:].bitcast(I32))
+        for a in range(2):
+            for q in range(4):
+                src, dst = LOAD_ROW[a] + 4 * q, 32 * q + PLANE_ROW[a]
+                if src != dst:
+                    nc.sync.dma_start(
+                        out=planes[dst : dst + 4, :].bitcast(I32), in_=planes[src : src + 4, :].bitcast(I32)
+                    )
+
+        assay_tab.append(keep.tile([P, T2], I32, name="assay_sc_listed", align_bytes=64))
+        nc.sync.dma_start(out=assay_tab[1][:], in_=words(tab2_words, 1))
+        w4_sc = keep.tile([P, N // 4], I32, name="frag_sc_listed", align_bytes=64)
+        nc.vector.memset(w4_sc[:], 0)
 
         def gather_frag(a, g):
             nc.vector.tensor_copy(
@@ -87,41 +97,37 @@ def tile_list_fragment_assay_screen_kernel(
                 frag_tab[a][:].bitcast(U32).indirect(frag_list[:, 32 * g : 32 * g + 32]),
             )
 
-        def gather_assay(a, h):
+        def gather_assay(a, lo, hi):
             nc.vector.tensor_copy(
-                assay[a][h][:], assay_tab[a][:].bitcast(U32).indirect(assay_list[:, 32 * h : 32 * h + 32])
+                assay[a][:, lo:hi], assay_tab[a][:].bitcast(U32).indirect(assay_list[:, lo // 16 : hi // 16])
             )
 
-        def gather_assay_chunk(c):
-            nc.vector.tensor_copy(
-                assay[1][0][:, CW * c : CW * (c + 1)],
-                assay_tab[1][:].bitcast(U32).indirect(assay_list[:, 16 * c : 16 * c + 16]),
-            )
-
-        gather_assay(0, 0)
-        gather_assay(0, 1)
-        nc.vector.tensor_copy(assay_sc[:], assay_tab_sc[:].bitcast(U8).indirect(assay_list[:]))
-        nc.vector.tensor_copy(frag_sc_listed[:], frag_tab_sc[:].bitcast(U8).indirect(frag_list[:]))
-        nc.vector.tensor_copy(
-            frag_sc[:].rearrange("p (g t m) -> p g t m", g=2, t=PACK),
-            frag_sc_listed[:].rearrange("p (g m t) -> p g t m", g=2, t=PACK),
-        )
+        gather_assay(0, 0, S2)
+        wn_raw = keep.tile([P, PACK, N], F32, name="assay_tab0", align_bytes=64)
+        nc.sync.dma_start(out=wn_raw[:], in_=wn.rearrange("(p t) n -> p t n", t=PACK))
+        for r in range(4):
+            nc.sync.dma_start(out=w4_sc[r:P:32, :], in_=w4_scales[0, r:16:4, :].bitcast(I32))
         gather_frag(0, 0)
         gather_frag(0, 1)
+        w4 = keep.tile([P, 2 * N], U8, name="frag_tab0", align_bytes=64)
+        nc.sync.dma_start(out=w4[:].bitcast(I32), in_=w4_words[0].bitcast(I32))
         gather_frag(1, 0)
         gather_frag(1, 1)
-        gather_assay_chunk(0)
-        gather_assay_chunk(1)
-        gather_assay(1, 1)
+        base_sb = keep.tile([P, N // P], F32, name="frag_tab1", align_bytes=64)
+        with nc.allow_non_contiguous_dma(reason="one bias value a partition"):
+            nc.sync.dma_start(out=base_sb[:], in_=base.rearrange("(c p) -> p c", p=P))
+        gather_assay(1, 0, CW)
+        gather_assay(1, CW, 2 * CW)
+        gather_assay(1, 2 * CW, S2)
 
         def a_pass(bank, a, c, g, t):
             col = KP * g + P * t
             nc.tensor.matmul_mx(
                 out=bank[:, t % 2, :],
                 lhsT=frag[a][g][:, P * t : P * t + P].bitcast(FP8X4),
-                lhsT_scale=frag_sc[FRAG_ROW[a] :, col : col + P],
-                rhs=assay[a][c // 2][:, CW * (c % 2) : CW * (c % 2 + 1)].bitcast(FP8X4),
-                rhs_scale=assay_sc[ASSAY_ROW[a] :, CW * c : CW * (c + 1)],
+                lhsT_scale=planes[PLANE_ROW[a] :, col : col + P],
+                rhs=assay[a][:, CW * c : CW * (c + 1)].bitcast(FP8X4),
+                rhs_scale=planes[PLANE_ROW[a] :, S + CW * c : S + CW * (c + 1)],
                 start=(a == 0),
                 stop=(a == 1),
             )

@@ -23,8 +23,8 @@ JW = 512
 RUN = 4
 CW = 256
 WN_SPLIT = 64
-PLANE_ROW = (0, 12)
-LOAD_ROW = (84, 12)
+PLANE_ROW = (0, 4)
+SPREAD = 4
 
 
 def tile_list_fragment_assay_screen_kernel(
@@ -47,6 +47,9 @@ def tile_list_fragment_assay_screen_kernel(
 
         nc.vector.memset(frag_tab_sc[:], 0)
         nc.vector.memset(assay_tab_sc[:], 0)
+        planes = [keep.tile([P, S + S2], U8, name="planes%d" % a, align_bytes=64) for a in range(2)]
+        for a in range(2):
+            nc.vector.memset(planes[a][:].bitcast(I32), 0)
         nc.vector.memset(warm[:, 0:1], 0.0)
         nc.scalar.activation(warm[:, 1:2], warm[:, 0:1], ACT.Square, bias=1.0)
 
@@ -58,8 +61,7 @@ def tile_list_fragment_assay_screen_kernel(
         nc.sync.dma_start(frag_list[:], offs)
         nc.sync.dma_start(out=assay_tab[0][:, :half], in_=words(tab2_words, 0)[:, :half])
         for window, rows in ((frag_tab_sc, tab_scales), (assay_tab_sc, tab2_scales)):
-            for a in range(2):
-                nc.sync.dma_start(out=window[LOAD_ROW[a] : LOAD_ROW[a] + 16, :], in_=rows[a].bitcast(I32))
+            nc.sync.dma_start(out=window[0:P:SPREAD, :], in_=rows.rearrange("a q t -> (a q) t").bitcast(I32))
         nc.sync.dma_start(out=assay_tab[0][:, half:], in_=words(tab2_words, 0)[:, half:])
         nc.sync.dma_start(out=frag_tab[0][:], in_=words(tab_words, 0))
         nc.sync.dma_start(out=fw_sb[:], in_=fw.rearrange("(g p t) -> p g t", g=2, t=PACK))
@@ -69,27 +71,29 @@ def tile_list_fragment_assay_screen_kernel(
         assay = [keep.tile([P, S2], U32, name="assay%d" % a, align_bytes=64) for a in range(2)]
         frag_sc_listed = keep.tile([P, S], U8, name="frag_sc_listed", align_bytes=64)
         assay_sc_listed = keep.tile([P, S2], U8, name="assay_sc_listed", align_bytes=64)
-        planes = keep.tile([P, S + S2], U8, name="planes", align_bytes=64)
+        staged = keep.tile([P, S + S2], U8, name="staged", align_bytes=64)
 
         nc.vector.tensor_copy(frag_sc_listed[:], frag_tab_sc[:].bitcast(U8).indirect(frag_list[:]))
         nc.vector.tensor_copy(assay_sc_listed[:], assay_tab_sc[:].bitcast(U8).indirect(assay_list[:]))
         nc.vector.tensor_copy(
-            planes[:, :S].rearrange("p (g t m) -> p g t m", g=2, t=PACK),
+            staged[:, :S].rearrange("p (g t m) -> p g t m", g=2, t=PACK),
             frag_sc_listed[:].rearrange("p (g m t) -> p g t m", g=2, t=PACK),
         )
-        nc.vector.tensor_copy(planes[:, S:].bitcast(I32), assay_sc_listed[:].bitcast(I32))
-        for a in range(2):
-            for q in range(4):
-                src, dst = LOAD_ROW[a] + 4 * q, 32 * q + PLANE_ROW[a]
-                if src != dst:
-                    nc.sync.dma_start(
-                        out=planes[dst : dst + 4, :].bitcast(I32), in_=planes[src : src + 4, :].bitcast(I32)
-                    )
+        nc.vector.tensor_copy(staged[:, S:].bitcast(I32), assay_sc_listed[:].bitcast(I32))
 
+        def carry(a, r):
+            src = SPREAD * (16 * a + r)
+            nc.sync.dma_start(
+                out=planes[a][PLANE_ROW[a] + r : P : 32, :].bitcast(I32),
+                in_=staged[src : 64 * (a + 1) : 4 * SPREAD, :].bitcast(I32),
+            )
+
+        for a, r in ((0, 0), (1, 0), (0, 1), (1, 1), (0, 2), (0, 3)):
+            carry(a, r)
         assay_tab.append(keep.tile([P, T2], I32, name="assay_sc_listed", align_bytes=64))
         nc.sync.dma_start(out=assay_tab[1][:], in_=words(tab2_words, 1))
-        w4_sc = keep.tile([P, N // 4], I32, name="frag_sc_listed", align_bytes=64)
-        nc.vector.memset(w4_sc[:], 0)
+        carry(1, 2)
+        carry(1, 3)
 
         def gather_frag(a, g):
             nc.vector.tensor_copy(
@@ -105,29 +109,31 @@ def tile_list_fragment_assay_screen_kernel(
         gather_assay(0, 0, S2)
         wn_raw = keep.tile([P, PACK, N], F32, name="assay_tab0", align_bytes=64)
         nc.sync.dma_start(out=wn_raw[:], in_=wn.rearrange("(p t) n -> p t n", t=PACK))
-        for r in range(4):
-            nc.sync.dma_start(out=w4_sc[r:P:32, :], in_=w4_scales[0, r:16:4, :].bitcast(I32))
         gather_frag(0, 0)
         gather_frag(0, 1)
         w4 = keep.tile([P, 2 * N], U8, name="frag_tab0", align_bytes=64)
         nc.sync.dma_start(out=w4[:].bitcast(I32), in_=w4_words[0].bitcast(I32))
         gather_frag(1, 0)
         gather_frag(1, 1)
-        base_sb = keep.tile([P, N // P], F32, name="frag_tab1", align_bytes=64)
-        with nc.allow_non_contiguous_dma(reason="one bias value a partition"):
-            nc.sync.dma_start(out=base_sb[:], in_=base.rearrange("(c p) -> p c", p=P))
+        w4_sc = keep.tile([P, N // 4], I32, name="frag_tab1", align_bytes=64)
+        nc.gpsimd.memset(w4_sc[:], 0)
+        for r in range(4):
+            nc.sync.dma_start(out=w4_sc[r:P:32, :], in_=w4_scales[0, r:16:4, :].bitcast(I32))
         gather_assay(1, 0, CW)
         gather_assay(1, CW, 2 * CW)
         gather_assay(1, 2 * CW, S2)
+        base_sb = keep.tile([P, N // P], F32, name="assay_sc_listed", align_bytes=64)
+        with nc.allow_non_contiguous_dma(reason="one bias value a partition"):
+            nc.sync.dma_start(out=base_sb[:], in_=base.rearrange("(c p) -> p c", p=P))
 
         def a_pass(bank, a, c, g, t):
             col = KP * g + P * t
             nc.tensor.matmul_mx(
                 out=bank[:, t % 2, :],
                 lhsT=frag[a][g][:, P * t : P * t + P].bitcast(FP8X4),
-                lhsT_scale=planes[PLANE_ROW[a] :, col : col + P],
+                lhsT_scale=planes[a][PLANE_ROW[a] :, col : col + P],
                 rhs=assay[a][:, CW * c : CW * (c + 1)].bitcast(FP8X4),
-                rhs_scale=planes[PLANE_ROW[a] :, S + CW * c : S + CW * (c + 1)],
+                rhs_scale=planes[a][PLANE_ROW[a] :, S + CW * c : S + CW * (c + 1)],
                 start=(a == 0),
                 stop=(a == 1),
             )

@@ -1,6 +1,7 @@
 from contextlib import ExitStack
 
 import concourse.mybir as mybir
+from concourse.masks import make_identity
 
 K, T, S, T2, S2, SO, N = 1024, 4096, 1024, 2048, 1024, 512, 512
 FLOPS = 2 * K * S * S2 + 2 * S * N * S2
@@ -20,9 +21,8 @@ P = 128
 PACK = 4
 KP = P * PACK
 JW = 512
-RUN = 4
 CW = 256
-WN_SPLIT = 64
+WN_STEP = 64
 PLANE_ROW = (0, 4)
 SPREAD = 4
 
@@ -34,7 +34,8 @@ def tile_list_fragment_assay_screen_kernel(
     with ExitStack() as ctx:
         keep = ctx.enter_context(tc.tile_pool(name="keep", bufs=1))
         ring = ctx.enter_context(tc.tile_pool(name="ring", bufs=5))
-        psum = ctx.enter_context(tc.psum_pool(name="psum", bufs=8))
+        psum = ctx.enter_context(tc.psum_pool(name="psum", bufs=7))
+        held = ctx.enter_context(tc.psum_pool(name="held", bufs=1))
 
         frag_list = keep.tile([P, S // 16], U16, name="frag_list")
         assay_list = keep.tile([P, S2 // 16], U16, name="assay_list")
@@ -42,7 +43,11 @@ def tile_list_fragment_assay_screen_kernel(
         assay_tab = [keep.tile([P, T2], I32, name="assay_tab0", align_bytes=64)]
         frag_tab_sc = keep.tile([P, T // 4], I32, name="frag_tab_sc", align_bytes=64)
         assay_tab_sc = keep.tile([P, T2 // 4], I32, name="assay_tab_sc", align_bytes=64)
-        fw_sb = keep.tile([P, 2, PACK], F32, name="fw_sb")
+        fw_sb = keep.tile([P, P], F32, name="fw_sb")
+        fw_rows = keep.tile([P, P], F32, name="fw_rows")
+        identity = keep.tile([P, P], F32, name="identity")
+        nc.gpsimd.memset(fw_sb[:], 0.0)
+        make_identity(nc, identity[:])
         warm = keep.tile([P, 2], F32, name="warm")
 
         nc.vector.memset(frag_tab_sc[:], 0)
@@ -64,7 +69,15 @@ def tile_list_fragment_assay_screen_kernel(
             nc.sync.dma_start(out=window[0:P:SPREAD, :], in_=rows.rearrange("a q t -> (a q) t").bitcast(I32))
         nc.sync.dma_start(out=assay_tab[0][:, half:], in_=words(tab2_words, 0)[:, half:])
         nc.sync.dma_start(out=frag_tab[0][:], in_=words(tab_words, 0))
-        nc.sync.dma_start(out=fw_sb[:], in_=fw.rearrange("(g p t) -> p g t", g=2, t=PACK))
+        nc.sync.dma_start(
+            out=fw_sb[:, : 2 * PACK].rearrange("p (g t) -> p g t", g=2),
+            in_=fw.rearrange("(g p t) -> p g t", g=2, t=PACK),
+        )
+        turned = psum.tile([P, P], F32, name="bank")
+        nc.tensor.transpose(turned[:], fw_sb[:], identity[:])
+        nc.scalar.copy(fw_rows[:], turned[:])
+        fw_ps = held.tile([P, P], F32, name="fw_ps")
+        nc.tensor.transpose(fw_ps[:], fw_rows[:], identity[:])
         nc.sync.dma_start(out=frag_tab[1][:], in_=words(tab_words, 1))
 
         frag = [[keep.tile([P, KP], U32, name="frag%d%d" % (a, g), align_bytes=64) for g in range(2)] for a in range(2)]
@@ -88,12 +101,12 @@ def tile_list_fragment_assay_screen_kernel(
                 in_=staged[src : 64 * (a + 1) : 4 * SPREAD, :].bitcast(I32),
             )
 
-        for a, r in ((0, 0), (1, 0), (0, 1), (1, 1), (0, 2), (0, 3)):
-            carry(a, r)
+        for r in range(4):
+            carry(0, r)
         assay_tab.append(keep.tile([P, T2], I32, name="assay_sc_listed", align_bytes=64))
         nc.sync.dma_start(out=assay_tab[1][:], in_=words(tab2_words, 1))
-        carry(1, 2)
-        carry(1, 3)
+        for r in range(4):
+            carry(1, r)
 
         def gather_frag(a, g):
             nc.vector.tensor_copy(
@@ -158,7 +171,7 @@ def tile_list_fragment_assay_screen_kernel(
             nc.vector.tensor_tensor(
                 z[:].rearrange("p (n u e) -> p n u e", u=2, e=2),
                 sq[:, :, lo : lo + width, :].rearrange("p u n e -> p n u e"),
-                fw_sb[:, g, :].rearrange("p (u e) -> p u e", u=2).unsqueeze(1).to_broadcast([P, width, 2, 2]),
+                fw_ps[:, PACK * g : PACK * (g + 1)].rearrange("p (u e) -> p u e", u=2).unsqueeze(1).to_broadcast([P, width, 2, 2]),
                 ALU.mult,
             )
             return z
@@ -221,23 +234,18 @@ def tile_list_fragment_assay_screen_kernel(
                     nc.sync.dma_start(out=out_tiles[:, rows, j0 : j0 + width], in_=res[:, rows, :])
 
         units = [(0, 0), (1, 0), (0, 1), (1, 1), (2, 0), (2, 1), (3, 0), (3, 1)]
-        opened = [a_open(c, g) for c, g in units[:4]]
-        sq = [a_close(opened[k], *units[k]) for k in range(4)]
+        sq = [a_close(a_open(*units[k]), *units[k]) for k in range(4)]
         wn_il = keep.tile([P, N * PACK], BF16, name="wn_il", align_bytes=64)
-        wn_dst = wn_il[:].rearrange("p (c i t) -> p c t i", i=RUN, t=PACK)
-        wn_src = wn_raw[:].rearrange("p t (c i) -> p c t i", i=RUN)
+        wn_dst = wn_il[:].rearrange("p (n t) -> p n t", t=PACK)
+        wn_src = wn_raw[:].rearrange("p t n -> p n t")
+        for n0 in range(0, N, WN_STEP):
+            cols = slice(n0, n0 + WN_STEP)
+            nc.gpsimd.tensor_scalar(wn_dst[:, cols], wn_src[:, cols], 1.0, 0.0, ALU.mult, ALU.add)
         z = []
         for k in range(7):
             z.append(weigh(sq[k], units[k][1], 0, CW))
             if k < 4:
                 sq.append(a_close(a_open(*units[k + 4]), *units[k + 4]))
-            if k == 0:
-                nc.vector.tensor_copy(wn_dst[:, :WN_SPLIT], wn_src[:, :WN_SPLIT])
-            if k == 1:
-                nc.scalar.copy(
-                    wn_il[:].rearrange("p (n t) -> p n t", t=PACK)[:, RUN * WN_SPLIT :],
-                    wn_raw[:].rearrange("p t n -> p n t")[:, RUN * WN_SPLIT :],
-                )
             if k > 0:
                 quantize_z(z[k - 1], *units[k - 1], 0, CW)
             if k == 4:
@@ -247,8 +255,8 @@ def tile_list_fragment_assay_screen_kernel(
                 y_block(2 * CW, CW, P, wq, (), 2)
         za = weigh(sq[7], 1, 0, P)
         quantize_z(z[6], 3, 0, 0, CW)
-        zb = weigh(sq[7], 1, P, P)
         quantize_z(za, 3, 1, 0, P)
-        quantize_z(zb, 3, 1, P, P)
         y_block(3 * CW, P, P, wq, (), 4)
+        zb = weigh(sq[7], 1, P, P)
+        quantize_z(zb, 3, 1, P, P)
         y_block(3 * CW + P, P, P, wq, (1, 3), 2)

@@ -23,6 +23,7 @@ KP = P * PACK
 JW = 512
 CW = 256
 WN_STEP = 64
+SHARE = 64
 PLANE_ROW = (0, 4)
 SPREAD = 4
 
@@ -34,6 +35,7 @@ def tile_list_fragment_assay_screen_kernel(
     with ExitStack() as ctx:
         keep = ctx.enter_context(tc.tile_pool(name="keep", bufs=1))
         ring = ctx.enter_context(tc.tile_pool(name="ring", bufs=5))
+        pair = ctx.enter_context(tc.tile_pool(name="pair", bufs=2))
         psum = ctx.enter_context(tc.psum_pool(name="psum", bufs=7))
         held = ctx.enter_context(tc.psum_pool(name="held", bufs=1))
 
@@ -43,10 +45,10 @@ def tile_list_fragment_assay_screen_kernel(
         assay_tab = [keep.tile([P, T2], I32, name="assay_tab0", align_bytes=64)]
         frag_tab_sc = keep.tile([P, T // 4], I32, name="frag_tab_sc", align_bytes=64)
         assay_tab_sc = keep.tile([P, T2 // 4], I32, name="assay_tab_sc", align_bytes=64)
-        fw_sb = keep.tile([P, P], F32, name="fw_sb")
-        fw_rows = keep.tile([P, P], F32, name="fw_rows")
+        fw_rows = keep.tile([P, KP], F32, name="fw_rows")
+        fw_sb = keep.tile([P, 2, PACK], F32, name="fw_sb")
         identity = keep.tile([P, P], F32, name="identity")
-        nc.gpsimd.memset(fw_sb[:], 0.0)
+        nc.gpsimd.memset(fw_rows[:], 0.0)
         make_identity(nc, identity[:])
         warm = keep.tile([P, 2], F32, name="warm")
 
@@ -69,15 +71,11 @@ def tile_list_fragment_assay_screen_kernel(
             nc.sync.dma_start(out=window[0:P:SPREAD, :], in_=rows.rearrange("a q t -> (a q) t").bitcast(I32))
         nc.sync.dma_start(out=assay_tab[0][:, half:], in_=words(tab2_words, 0)[:, half:])
         nc.sync.dma_start(out=frag_tab[0][:], in_=words(tab_words, 0))
-        nc.sync.dma_start(
-            out=fw_sb[:, : 2 * PACK].rearrange("p (g t) -> p g t", g=2),
-            in_=fw.rearrange("(g p t) -> p g t", g=2, t=PACK),
-        )
-        turned = psum.tile([P, P], F32, name="bank")
-        nc.tensor.transpose(turned[:], fw_sb[:], identity[:])
-        nc.scalar.copy(fw_rows[:], turned[:])
-        fw_ps = held.tile([P, P], F32, name="fw_ps")
-        nc.tensor.transpose(fw_ps[:], fw_rows[:], identity[:])
+        nc.sync.dma_start(out=fw_rows[0:2, :], in_=fw.rearrange("(g i) -> g i", g=2))
+        fw_ps = held.tile([P, PACK, P], F32, name="fw_ps")
+        for t in range(PACK):
+            nc.tensor.transpose(fw_ps[:, t, :], fw_rows[:, t:KP:PACK], identity[:])
+        nc.scalar.copy(fw_sb[:], fw_ps[:, :, 0:2].rearrange("p t g -> p g t"))
         nc.sync.dma_start(out=frag_tab[1][:], in_=words(tab_words, 1))
 
         frag = [[keep.tile([P, KP], U32, name="frag%d%d" % (a, g), align_bytes=64) for g in range(2)] for a in range(2)]
@@ -166,14 +164,20 @@ def tile_list_fragment_assay_screen_kernel(
                 nc.scalar.activation(sq[:, u], banks[u][:].rearrange("p e n -> p n e"), ACT.Square, bias=1.0)
             return sq
 
-        def weigh(sq, g, lo, width):
-            z = ring.tile([P, width * PACK], BF16, name="z", align_bytes=64)
-            nc.vector.tensor_tensor(
-                z[:].rearrange("p (n u e) -> p n u e", u=2, e=2),
-                sq[:, :, lo : lo + width, :].rearrange("p u n e -> p n u e"),
-                fw_ps[:, PACK * g : PACK * (g + 1)].rearrange("p (u e) -> p u e", u=2).unsqueeze(1).to_broadcast([P, width, 2, 2]),
-                ALU.mult,
-            )
+        def weigh(sq, g, lo, width, shared):
+            z = pair.tile([P, width * PACK], BF16, name="z", align_bytes=64)
+            own = width - shared
+            for engine, weights, n0, n1 in (
+                (nc.vector, fw_ps[:, :, g], 0, own),
+                (nc.gpsimd, fw_sb[:, g, :], own, width),
+            ):
+                if n1 > n0:
+                    engine.tensor_tensor(
+                        z[:, PACK * n0 : PACK * n1].rearrange("p (n u e) -> p n u e", u=2, e=2),
+                        sq[:, :, lo + n0 : lo + n1, :].rearrange("p u n e -> p n u e"),
+                        weights.rearrange("p (u e) -> p u e", u=2).unsqueeze(1).to_broadcast([P, n1 - n0, 2, 2]),
+                        ALU.mult,
+                    )
             return z
 
         zq = {}
@@ -243,7 +247,7 @@ def tile_list_fragment_assay_screen_kernel(
             nc.gpsimd.tensor_scalar(wn_dst[:, cols], wn_src[:, cols], 1.0, 0.0, ALU.mult, ALU.add)
         z = []
         for k in range(7):
-            z.append(weigh(sq[k], units[k][1], 0, CW))
+            z.append(weigh(sq[k], units[k][1], 0, CW, SHARE if k >= 3 else 0))
             if k < 4:
                 sq.append(a_close(a_open(*units[k + 4]), *units[k + 4]))
             if k > 0:
@@ -253,10 +257,10 @@ def tile_list_fragment_assay_screen_kernel(
                 y_block(0, JW, JW, wq, (), 1)
             if k == 6:
                 y_block(2 * CW, CW, P, wq, (), 2)
-        za = weigh(sq[7], 1, 0, P)
+        za = weigh(sq[7], 1, 0, P, SHARE // 2)
         quantize_z(z[6], 3, 0, 0, CW)
         quantize_z(za, 3, 1, 0, P)
         y_block(3 * CW, P, P, wq, (), 4)
-        zb = weigh(sq[7], 1, P, P)
+        zb = weigh(sq[7], 1, P, P, SHARE // 2)
         quantize_z(zb, 3, 1, P, P)
         y_block(3 * CW + P, P, P, wq, (1, 3), 2)

@@ -133,7 +133,7 @@ def tile_list_fragment_assay_screen_kernel(
         gather_assay(1, 0, CW)
         gather_assay(1, CW, 2 * CW)
         gather_assay(1, 2 * CW, S2)
-        base_sb = keep.tile([P, N // P], F32, name="assay_sc_listed", align_bytes=64)
+        base_sb = keep.tile([P, N // P], F32, name="staged", align_bytes=64)
         with nc.allow_non_contiguous_dma(reason="one bias value a partition"):
             nc.sync.dma_start(out=base_sb[:], in_=base.rearrange("(c p) -> p c", p=P))
 
@@ -239,7 +239,7 @@ def tile_list_fragment_assay_screen_kernel(
 
         units = [(0, 0), (1, 0), (0, 1), (1, 1), (2, 0), (2, 1), (3, 0), (3, 1)]
         sq = [a_close(a_open(*units[k]), *units[k]) for k in range(4)]
-        wn_il = keep.tile([P, N * PACK], BF16, name="wn_il", align_bytes=64)
+        wn_il = keep.tile([P, N * PACK], BF16, name="assay_sc_listed", align_bytes=64)
         wn_dst = wn_il[:].rearrange("p (n t) -> p n t", t=PACK)
         wn_src = wn_raw[:].rearrange("p t n -> p n t")
         for n0 in range(0, N, WN_STEP):

@@ -3,7 +3,7 @@ from contextlib import ExitStack
 import concourse.mybir as mybir
 from concourse.masks import make_identity
 
-K, T, S, T2, S2, SO, N = 1024, 4096, 1024, 2048, 1024, 512, 512
+K, T, S, T2, S2, N = 1024, 4096, 1024, 2048, 1024, 512
 FLOPS = 2 * K * S * S2 + 2 * S * N * S2
 
 F32 = mybir.dt.float32
@@ -19,13 +19,19 @@ ALU = mybir.AluOpType
 
 P = 128
 PACK = 4
-KP = P * PACK
-JW = 512
-CW = 256
+PASS = P * PACK
+STRIPE = 16
+QUAD = 32
+ROWS = 4
+BANK = 512
+CHUNK = 256
+SPREAD = 4
+PLANE_ROW = (0, 4)
 WN_STEP = 64
 SHARE = 64
-PLANE_ROW = (0, 4)
-SPREAD = 4
+SHARE_FROM = 3
+SHARE_LAST = 16
+AHEAD = 4
 
 
 def tile_list_fragment_assay_screen_kernel(
@@ -34,51 +40,49 @@ def tile_list_fragment_assay_screen_kernel(
     nc = tc.nc
     with ExitStack() as ctx:
         keep = ctx.enter_context(tc.tile_pool(name="keep", bufs=1))
-        ring = ctx.enter_context(tc.tile_pool(name="ring", bufs=5))
-        pair = ctx.enter_context(tc.tile_pool(name="pair", bufs=2))
+        squares = ctx.enter_context(tc.tile_pool(name="squares", bufs=AHEAD + 1))
+        weighed = ctx.enter_context(tc.tile_pool(name="weighed", bufs=2))
         psum = ctx.enter_context(tc.psum_pool(name="psum", bufs=7))
         held = ctx.enter_context(tc.psum_pool(name="held", bufs=1))
 
-        frag_list = keep.tile([P, S // 16], U16, name="frag_list")
-        assay_list = keep.tile([P, S2 // 16], U16, name="assay_list")
+        frag_list = keep.tile([P, S // STRIPE], U16, name="frag_list")
+        assay_list = keep.tile([P, S2 // STRIPE], U16, name="assay_list")
         frag_tab = [keep.tile([P, T], I32, name="frag_tab%d" % a, align_bytes=64) for a in range(2)]
         assay_tab = [keep.tile([P, T2], I32, name="assay_tab0", align_bytes=64)]
         frag_tab_sc = keep.tile([P, T // 4], I32, name="frag_tab_sc", align_bytes=64)
         assay_tab_sc = keep.tile([P, T2 // 4], I32, name="assay_tab_sc", align_bytes=64)
-        fw_rows = keep.tile([P, KP], F32, name="fw_rows")
-        fw_sb = keep.tile([P, 2, PACK], F32, name="fw_sb")
+        fw_rows = keep.tile([P, PASS], F32, name="fw_rows")
+        fw_sb = keep.tile([P, 2 * PACK], F32, name="fw_sb")
         identity = keep.tile([P, P], F32, name="identity")
+
         nc.gpsimd.memset(fw_rows[:], 0.0)
         make_identity(nc, identity[:])
-        warm = keep.tile([P, 2], F32, name="warm")
-
         nc.vector.memset(frag_tab_sc[:], 0)
         nc.vector.memset(assay_tab_sc[:], 0)
         planes = [keep.tile([P, S + S2], U8, name="planes%d" % a, align_bytes=64) for a in range(2)]
         for a in range(2):
             nc.vector.memset(planes[a][:].bitcast(I32), 0)
-        nc.vector.memset(warm[:, 0:1], 0.0)
-        nc.scalar.activation(warm[:, 1:2], warm[:, 0:1], ACT.Square, bias=1.0)
 
         def words(tab, a):
             return tab[a].rearrange("p t i -> p (t i)").bitcast(I32)
 
         half = T2 // 2
-        nc.sync.dma_start(assay_list[:], offs2)
-        nc.sync.dma_start(frag_list[:], offs)
         nc.sync.dma_start(out=assay_tab[0][:, :half], in_=words(tab2_words, 0)[:, :half])
+        nc.sync.dma_start(frag_list[:], offs)
+        nc.sync.dma_start(assay_list[:], offs2)
         for window, rows in ((frag_tab_sc, tab_scales), (assay_tab_sc, tab2_scales)):
             nc.sync.dma_start(out=window[0:P:SPREAD, :], in_=rows.rearrange("a q t -> (a q) t").bitcast(I32))
         nc.sync.dma_start(out=assay_tab[0][:, half:], in_=words(tab2_words, 0)[:, half:])
         nc.sync.dma_start(out=frag_tab[0][:], in_=words(tab_words, 0))
+
         nc.sync.dma_start(out=fw_rows[0:2, :], in_=fw.rearrange("(g i) -> g i", g=2))
-        fw_ps = held.tile([P, PACK, P], F32, name="fw_ps")
+        fw_ps = held.tile([P, BANK], F32, name="fw_ps")
         for t in range(PACK):
-            nc.tensor.transpose(fw_ps[:, t, :], fw_rows[:, t:KP:PACK], identity[:])
-        nc.scalar.copy(fw_sb[:], fw_ps[:, :, 0:2].rearrange("p t g -> p g t"))
+            nc.tensor.transpose(fw_ps[:, t:BANK:PACK], fw_rows[:, t:PASS:PACK], identity[:])
+        nc.scalar.activation(fw_sb[:], fw_ps[:, : 2 * PACK], ACT.Identity)
         nc.sync.dma_start(out=frag_tab[1][:], in_=words(tab_words, 1))
 
-        frag = [[keep.tile([P, KP], U32, name="frag%d%d" % (a, g), align_bytes=64) for g in range(2)] for a in range(2)]
+        frag = [[keep.tile([P, PASS], U32, name="frag%d%d" % (a, g), align_bytes=64) for g in range(2)] for a in range(2)]
         assay = [keep.tile([P, S2], U32, name="assay%d" % a, align_bytes=64) for a in range(2)]
         frag_sc_listed = keep.tile([P, S], U8, name="frag_sc_listed", align_bytes=64)
         assay_sc_listed = keep.tile([P, S2], U8, name="assay_sc_listed", align_bytes=64)
@@ -92,29 +96,28 @@ def tile_list_fragment_assay_screen_kernel(
         )
         nc.vector.tensor_copy(staged[:, S:].bitcast(I32), assay_sc_listed[:].bitcast(I32))
 
-        def carry(a, r):
-            src = SPREAD * (16 * a + r)
-            nc.sync.dma_start(
-                out=planes[a][PLANE_ROW[a] + r : P : 32, :].bitcast(I32),
-                in_=staged[src : 64 * (a + 1) : 4 * SPREAD, :].bitcast(I32),
-            )
+        def carry_scale_rows(a):
+            first = SPREAD * 16 * a
+            for r in range(ROWS):
+                nc.sync.dma_start(
+                    out=planes[a][PLANE_ROW[a] + r : P : QUAD, :].bitcast(I32),
+                    in_=staged[first + SPREAD * r : first + SPREAD * 16 : SPREAD * ROWS, :].bitcast(I32),
+                )
 
-        for r in range(4):
-            carry(0, r)
+        carry_scale_rows(0)
         assay_tab.append(keep.tile([P, T2], I32, name="assay_sc_listed", align_bytes=64))
         nc.sync.dma_start(out=assay_tab[1][:], in_=words(tab2_words, 1))
-        for r in range(4):
-            carry(1, r)
+        carry_scale_rows(1)
 
         def gather_frag(a, g):
             nc.vector.tensor_copy(
                 frag[a][g][:].rearrange("p (t m) -> p m t", t=PACK),
-                frag_tab[a][:].bitcast(U32).indirect(frag_list[:, 32 * g : 32 * g + 32]),
+                frag_tab[a][:].bitcast(U32).indirect(frag_list[:, PASS * g // STRIPE : PASS * (g + 1) // STRIPE]),
             )
 
         def gather_assay(a, lo, hi):
             nc.vector.tensor_copy(
-                assay[a][:, lo:hi], assay_tab[a][:].bitcast(U32).indirect(assay_list[:, lo // 16 : hi // 16])
+                assay[a][:, lo:hi], assay_tab[a][:].bitcast(U32).indirect(assay_list[:, lo // STRIPE : hi // STRIPE])
             )
 
         gather_assay(0, 0, S2)
@@ -128,35 +131,32 @@ def tile_list_fragment_assay_screen_kernel(
         gather_frag(1, 1)
         w4_sc = keep.tile([P, N // 4], I32, name="frag_tab1", align_bytes=64)
         nc.gpsimd.memset(w4_sc[:], 0)
-        for r in range(4):
-            nc.sync.dma_start(out=w4_sc[r:P:32, :], in_=w4_scales[0, r:16:4, :].bitcast(I32))
-        gather_assay(1, 0, CW)
-        gather_assay(1, CW, 2 * CW)
-        gather_assay(1, 2 * CW, S2)
+        for r in range(ROWS):
+            nc.sync.dma_start(out=w4_sc[r:P:QUAD, :], in_=w4_scales[0, r:16:ROWS, :].bitcast(I32))
+        gather_assay(1, 0, CHUNK)
+        gather_assay(1, CHUNK, 2 * CHUNK)
+        gather_assay(1, 2 * CHUNK, S2)
         base_sb = keep.tile([P, N // P], F32, name="staged", align_bytes=64)
         with nc.allow_non_contiguous_dma(reason="one bias value a partition"):
-            nc.sync.dma_start(out=base_sb[:], in_=base.rearrange("(c p) -> p c", p=P))
+            nc.sync.dma_start(out=base_sb[:], in_=base.rearrange("(r p) -> p r", p=P))
 
         def a_pass(bank, a, c, g, t):
-            col = KP * g + P * t
+            col = PASS * g + P * t
             nc.tensor.matmul_mx(
                 out=bank[:, t % 2, :],
                 lhsT=frag[a][g][:, P * t : P * t + P].bitcast(FP8X4),
                 lhsT_scale=planes[a][PLANE_ROW[a] :, col : col + P],
-                rhs=assay[a][:, CW * c : CW * (c + 1)].bitcast(FP8X4),
-                rhs_scale=planes[a][PLANE_ROW[a] :, S + CW * c : S + CW * (c + 1)],
+                rhs=assay[a][:, CHUNK * c : CHUNK * (c + 1)].bitcast(FP8X4),
+                rhs_scale=planes[a][PLANE_ROW[a] :, S + CHUNK * c : S + CHUNK * (c + 1)],
                 start=(a == 0),
                 stop=(a == 1),
             )
 
-        def a_open(c, g):
-            banks = [psum.tile([P, 2, CW], F32, name="bank") for u in range(2)]
+        def square_unit(c, g):
+            banks = [psum.tile([P, 2, CHUNK], F32, name="bank") for u in range(2)]
             for u in range(2):
                 a_pass(banks[u], 0, c, g, 2 * u)
-            return banks
-
-        def a_close(banks, c, g):
-            sq = ring.tile([P, 2, CW, 2], F32, name="sq", align_bytes=64)
+            sq = squares.tile([P, 2, CHUNK, 2], F32, name="sq", align_bytes=64)
             for u in range(2):
                 a_pass(banks[u], 1, c, g, 2 * u)
                 a_pass(banks[u], 0, c, g, 2 * u + 1)
@@ -165,17 +165,17 @@ def tile_list_fragment_assay_screen_kernel(
             return sq
 
         def weigh(sq, g, lo, width, shared):
-            z = pair.tile([P, width * PACK], BF16, name="z", align_bytes=64)
+            z = weighed.tile([P, width * PACK], BF16, name="z", align_bytes=64)
             own = width - shared
-            for engine, weights, n0, n1 in (
-                (nc.vector, fw_ps[:, :, g], 0, own),
-                (nc.gpsimd, fw_sb[:, g, :], own, width),
-            ):
+            for engine, weights, n0, n1 in ((nc.vector, fw_ps, 0, own), (nc.gpsimd, fw_sb, own, width)):
                 if n1 > n0:
                     engine.tensor_tensor(
                         z[:, PACK * n0 : PACK * n1].rearrange("p (n u e) -> p n u e", u=2, e=2),
                         sq[:, :, lo + n0 : lo + n1, :].rearrange("p u n e -> p n u e"),
-                        weights.rearrange("p (u e) -> p u e", u=2).unsqueeze(1).to_broadcast([P, n1 - n0, 2, 2]),
+                        weights[:, PACK * g : PACK * (g + 1)]
+                        .rearrange("p (u e) -> p u e", u=2)
+                        .unsqueeze(1)
+                        .to_broadcast([P, n1 - n0, 2, 2]),
                         ALU.mult,
                     )
             return z
@@ -184,19 +184,19 @@ def tile_list_fragment_assay_screen_kernel(
         for h in range(2):
             for g in range(2):
                 zq[h, g] = (
-                    keep.tile([P, JW], U32, name="z_codes%d%d" % (h, g), align_bytes=64),
-                    keep.tile([P, JW], U8, name="z_scales%d%d" % (h, g), align_bytes=64),
+                    keep.tile([P, BANK], U32, name="z_codes%d%d" % (h, g), align_bytes=64),
+                    keep.tile([P, BANK], U8, name="z_scales%d%d" % (h, g), align_bytes=64),
                 )
 
         def quantize_z(z, c, g, lo, width):
             codes, scales = zq[c // 2, g]
-            cols = slice(CW * (c % 2) + lo, CW * (c % 2) + lo + width)
+            cols = slice(CHUNK * (c % 2) + lo, CHUNK * (c % 2) + lo + width)
             nc.vector.quantize_mx(out=codes[:, cols].bitcast(FP8X4), scales=scales[:, cols], in_=z[:])
 
-        def quantize(src, label):
-            codes = keep.tile([P, JW], U32, name=label + "_codes", align_bytes=64)
-            scales = keep.tile([P, JW], U8, name=label + "_scales", align_bytes=64)
-            nc.vector.quantize_mx(out=codes[:].bitcast(FP8X4), scales=scales[:], in_=src[:])
+        def quantize_wn(wn_il):
+            codes = keep.tile([P, N], U32, name="wn_codes", align_bytes=64)
+            scales = keep.tile([P, N], U8, name="wn_scales", align_bytes=64)
+            nc.vector.quantize_mx(out=codes[:].bitcast(FP8X4), scales=scales[:], in_=wn_il[:])
             return codes, scales
 
         def y_pass(dst, g, r, h, cols, wq):
@@ -219,7 +219,7 @@ def tile_list_fragment_assay_screen_kernel(
         out_tiles = out.rearrange("(r p) j -> p r j", p=P)
 
         def y_block(j0, width, group, wq, on_vector, per_store):
-            h, off = divmod(j0, JW)
+            h, off = divmod(j0, BANK)
             banks = [psum.tile([P, width], F32, name="bank") for r in range(N // P)]
             res = keep.tile([P, N // P, width], F32, name="res%d" % j0, align_bytes=64)
             for r in range(N // P):
@@ -235,32 +235,38 @@ def tile_list_fragment_assay_screen_kernel(
                     nc.scalar.activation(res[:, r, :], banks[r][:], ACT.Identity, bias=base_sb[:, r : r + 1])
                 if (r + 1) % per_store == 0:
                     rows = slice(r + 1 - per_store, r + 1)
-                    nc.sync.dma_start(out=out_tiles[:, rows, j0 : j0 + width], in_=res[:, rows, :])
+                    queue = nc.scalar if on_vector and r not in on_vector else nc.sync
+                    queue.dma_start(out=out_tiles[:, rows, j0 : j0 + width], in_=res[:, rows, :])
 
-        units = [(0, 0), (1, 0), (0, 1), (1, 1), (2, 0), (2, 1), (3, 0), (3, 1)]
-        sq = [a_close(a_open(*units[k]), *units[k]) for k in range(4)]
+        units = [(c, g) for g in range(2) for c in range(2)] + [(c, g) for c in range(2, 4) for g in range(2)]
+        last = len(units) - 1
+        sq = [square_unit(*units[k]) for k in range(AHEAD)]
+
         wn_il = keep.tile([P, N * PACK], BF16, name="assay_sc_listed", align_bytes=64)
         wn_dst = wn_il[:].rearrange("p (n t) -> p n t", t=PACK)
         wn_src = wn_raw[:].rearrange("p t n -> p n t")
         for n0 in range(0, N, WN_STEP):
             cols = slice(n0, n0 + WN_STEP)
             nc.gpsimd.tensor_scalar(wn_dst[:, cols], wn_src[:, cols], 1.0, 0.0, ALU.mult, ALU.add)
+
         z = []
-        for k in range(7):
-            z.append(weigh(sq[k], units[k][1], 0, CW, SHARE if k >= 3 else 0))
-            if k < 4:
-                sq.append(a_close(a_open(*units[k + 4]), *units[k + 4]))
+        for k in range(last):
+            z.append(weigh(sq[k], units[k][1], 0, CHUNK, SHARE if k >= SHARE_FROM else 0))
+            if k + AHEAD <= last:
+                sq.append(square_unit(*units[k + AHEAD]))
             if k > 0:
-                quantize_z(z[k - 1], *units[k - 1], 0, CW)
+                quantize_z(z[k - 1], *units[k - 1], 0, CHUNK)
             if k == 4:
-                wq = quantize(wn_il, "wn")
-                y_block(0, JW, JW, wq, (), 1)
+                wq = quantize_wn(wn_il)
+                y_block(0, BANK, BANK, wq, (), 1)
             if k == 6:
-                y_block(2 * CW, CW, P, wq, (), 2)
-        za = weigh(sq[7], 1, 0, P, SHARE // 2)
-        quantize_z(z[6], 3, 0, 0, CW)
-        quantize_z(za, 3, 1, 0, P)
-        y_block(3 * CW, P, P, wq, (), 4)
-        zb = weigh(sq[7], 1, P, P, SHARE // 2)
-        quantize_z(zb, 3, 1, P, P)
-        y_block(3 * CW + P, P, P, wq, (1, 3), 2)
+                y_block(2 * CHUNK, CHUNK, P, wq, (), 2)
+
+        c, g = units[last]
+        z_first = weigh(sq[last], g, 0, P, SHARE_LAST)
+        quantize_z(z[last - 1], *units[last - 1], 0, CHUNK)
+        quantize_z(z_first, c, g, 0, P)
+        y_block(c * CHUNK, P, P, wq, (), 4)
+        z_second = weigh(sq[last], g, P, P, 0)
+        quantize_z(z_second, c, g, P, P)
+        y_block(c * CHUNK + P, P, P, wq, (0, 1), 2)

@@ -25,12 +25,13 @@ QUAD = 32
 ROWS = 4
 BANK = 512
 CHUNK = 256
-SPREAD = 4
+LOADED = 96
 PLANE_ROW = (0, 4)
-WN_STEP = 64
+WN_STEP = 256
 SHARE = 64
 SHARE_FROM = 3
 SHARE_LAST = 16
+JOINT = 1
 AHEAD = 4
 
 
@@ -57,8 +58,8 @@ def tile_list_fragment_assay_screen_kernel(
 
         nc.gpsimd.memset(fw_rows[:], 0.0)
         make_identity(nc, identity[:])
-        nc.vector.memset(frag_tab_sc[:], 0)
-        nc.vector.memset(assay_tab_sc[:], 0)
+        nc.vector.memset(assay_tab_sc[:LOADED, :], 0)
+        nc.vector.memset(frag_tab_sc[:LOADED, :], 0)
         planes = [keep.tile([P, S + S2], U8, name="planes%d" % a, align_bytes=64) for a in range(2)]
         for a in range(2):
             nc.vector.memset(planes[a][:].bitcast(I32), 0)
@@ -66,13 +67,13 @@ def tile_list_fragment_assay_screen_kernel(
         def words(tab, a):
             return tab[a].rearrange("p t i -> p (t i)").bitcast(I32)
 
-        half = T2 // 2
-        nc.sync.dma_start(out=assay_tab[0][:, :half], in_=words(tab2_words, 0)[:, :half])
-        nc.sync.dma_start(frag_list[:], offs)
-        nc.sync.dma_start(assay_list[:], offs2)
-        for window, rows in ((frag_tab_sc, tab_scales), (assay_tab_sc, tab2_scales)):
-            nc.sync.dma_start(out=window[0:P:SPREAD, :], in_=rows.rearrange("a q t -> (a q) t").bitcast(I32))
-        nc.sync.dma_start(out=assay_tab[0][:, half:], in_=words(tab2_words, 0)[:, half:])
+        for listed, entries, window, rows in (
+            (assay_list, offs2, assay_tab_sc, tab2_scales),
+            (frag_list, offs, frag_tab_sc, tab_scales),
+        ):
+            nc.sync.dma_start(listed[:], entries)
+            nc.sync.dma_start(out=window[LOADED:, :], in_=rows.rearrange("a q t -> (a q) t").bitcast(I32))
+        nc.sync.dma_start(out=assay_tab[0][:], in_=words(tab2_words, 0))
         nc.sync.dma_start(out=frag_tab[0][:], in_=words(tab_words, 0))
 
         nc.sync.dma_start(out=fw_rows[0:2, :], in_=fw.rearrange("(g i) -> g i", g=2))
@@ -88,24 +89,24 @@ def tile_list_fragment_assay_screen_kernel(
         assay_sc_listed = keep.tile([P, S2], U8, name="assay_sc_listed", align_bytes=64)
         staged = keep.tile([P, S + S2], U8, name="staged", align_bytes=64)
 
-        nc.vector.tensor_copy(frag_sc_listed[:], frag_tab_sc[:].bitcast(U8).indirect(frag_list[:]))
         nc.vector.tensor_copy(assay_sc_listed[:], assay_tab_sc[:].bitcast(U8).indirect(assay_list[:]))
+        nc.vector.tensor_copy(frag_sc_listed[:], frag_tab_sc[:].bitcast(U8).indirect(frag_list[:]))
+        nc.vector.tensor_copy(staged[:, S:].bitcast(I32), assay_sc_listed[:].bitcast(I32))
         nc.vector.tensor_copy(
             staged[:, :S].rearrange("p (g t m) -> p g t m", g=2, t=PACK),
             frag_sc_listed[:].rearrange("p (g m t) -> p g t m", g=2, t=PACK),
         )
-        nc.vector.tensor_copy(staged[:, S:].bitcast(I32), assay_sc_listed[:].bitcast(I32))
 
         def carry_scale_rows(a):
-            first = SPREAD * 16 * a
+            first = LOADED + 16 * a
             for r in range(ROWS):
                 nc.sync.dma_start(
                     out=planes[a][PLANE_ROW[a] + r : P : QUAD, :].bitcast(I32),
-                    in_=staged[first + SPREAD * r : first + SPREAD * 16 : SPREAD * ROWS, :].bitcast(I32),
+                    in_=staged[first + r : first + 16 : ROWS, :].bitcast(I32),
                 )
 
         carry_scale_rows(0)
-        assay_tab.append(keep.tile([P, T2], I32, name="assay_sc_listed", align_bytes=64))
+        assay_tab.append(keep.tile([P, T2], I32, name="frag_sc_listed", align_bytes=64))
         nc.sync.dma_start(out=assay_tab[1][:], in_=words(tab2_words, 1))
         carry_scale_rows(1)
 
@@ -140,7 +141,7 @@ def tile_list_fragment_assay_screen_kernel(
         with nc.allow_non_contiguous_dma(reason="one bias value a partition"):
             nc.sync.dma_start(out=base_sb[:], in_=base.rearrange("(r p) -> p r", p=P))
 
-        def a_pass(bank, a, c, g, t):
+        def a_pass(bank, a, c, g, t, joint):
             col = PASS * g + P * t
             nc.tensor.matmul_mx(
                 out=bank[:, t % 2, :],
@@ -148,24 +149,27 @@ def tile_list_fragment_assay_screen_kernel(
                 lhsT_scale=planes[a][PLANE_ROW[a] :, col : col + P],
                 rhs=assay[a][:, CHUNK * c : CHUNK * (c + 1)].bitcast(FP8X4),
                 rhs_scale=planes[a][PLANE_ROW[a] :, S + CHUNK * c : S + CHUNK * (c + 1)],
-                start=(a == 0),
-                stop=(a == 1),
+                start=(a == 0 and not (joint and t % 2 == 1)),
+                stop=(a == 1 and not (joint and t % 2 == 0)),
             )
 
-        def square_unit(c, g):
+        def square_unit(c, g, joint=False):
             banks = [psum.tile([P, 2, CHUNK], F32, name="bank") for u in range(2)]
-            for u in range(2):
-                a_pass(banks[u], 0, c, g, 2 * u)
+            for t in range(0, PACK, 1 if joint else 2):
+                a_pass(banks[t // 2], 0, c, g, t, joint)
             sq = squares.tile([P, 2, CHUNK, 2], F32, name="sq", align_bytes=64)
             for u in range(2):
-                a_pass(banks[u], 1, c, g, 2 * u)
-                a_pass(banks[u], 0, c, g, 2 * u + 1)
-                a_pass(banks[u], 1, c, g, 2 * u + 1)
+                a_pass(banks[u], 1, c, g, 2 * u, joint)
+                if not joint:
+                    a_pass(banks[u], 0, c, g, 2 * u + 1, joint)
+                a_pass(banks[u], 1, c, g, 2 * u + 1, joint)
                 nc.scalar.activation(sq[:, u], banks[u][:].rearrange("p e n -> p n e"), ACT.Square, bias=1.0)
             return sq
 
-        def weigh(sq, g, lo, width, shared):
-            z = weighed.tile([P, width * PACK], BF16, name="z", align_bytes=64)
+        def z_tile(width):
+            return weighed.tile([P, width * PACK], BF16, name="z", align_bytes=64)
+
+        def weigh(z, sq, g, lo, width, shared):
             own = width - shared
             for engine, weights, n0, n1 in ((nc.vector, fw_ps, 0, own), (nc.gpsimd, fw_sb, own, width)):
                 if n1 > n0:
@@ -191,7 +195,7 @@ def tile_list_fragment_assay_screen_kernel(
         def quantize_z(z, c, g, lo, width):
             codes, scales = zq[c // 2, g]
             cols = slice(CHUNK * (c % 2) + lo, CHUNK * (c % 2) + lo + width)
-            nc.vector.quantize_mx(out=codes[:, cols].bitcast(FP8X4), scales=scales[:, cols], in_=z[:])
+            nc.vector.quantize_mx(out=codes[:, cols].bitcast(FP8X4), scales=scales[:, cols], in_=z)
 
         def quantize_wn(wn_il):
             codes = keep.tile([P, N], U32, name="wn_codes", align_bytes=64)
@@ -240,21 +244,25 @@ def tile_list_fragment_assay_screen_kernel(
 
         units = [(c, g) for g in range(2) for c in range(2)] + [(c, g) for c in range(2, 4) for g in range(2)]
         last = len(units) - 1
-        sq = [square_unit(*units[k]) for k in range(AHEAD)]
+        sq = [square_unit(*units[k], joint=k < JOINT) for k in range(AHEAD)]
 
-        wn_il = keep.tile([P, N * PACK], BF16, name="assay_sc_listed", align_bytes=64)
+        wn_il = keep.tile([P, N * PACK], BF16, name="frag_sc_listed", align_bytes=64)
         wn_dst = wn_il[:].rearrange("p (n t) -> p n t", t=PACK)
         wn_src = wn_raw[:].rearrange("p t n -> p n t")
         for n0 in range(0, N, WN_STEP):
             cols = slice(n0, n0 + WN_STEP)
             nc.gpsimd.tensor_scalar(wn_dst[:, cols], wn_src[:, cols], 1.0, 0.0, ALU.mult, ALU.add)
 
+        pair = z_tile(2 * CHUNK)
         z = []
         for k in range(last):
-            z.append(weigh(sq[k], units[k][1], 0, CHUNK, SHARE if k >= SHARE_FROM else 0))
+            dst = pair[:, PACK * CHUNK * k : PACK * CHUNK * (k + 1)] if k < 2 else z_tile(CHUNK)[:]
+            z.append(weigh(dst, sq[k], units[k][1], 0, CHUNK, SHARE if k >= SHARE_FROM else 0))
             if k + AHEAD <= last:
                 sq.append(square_unit(*units[k + AHEAD]))
-            if k > 0:
+            if k == 2:
+                quantize_z(pair[:], *units[0], 0, 2 * CHUNK)
+            if k > 2:
                 quantize_z(z[k - 1], *units[k - 1], 0, CHUNK)
             if k == 4:
                 wq = quantize_wn(wn_il)
@@ -263,10 +271,10 @@ def tile_list_fragment_assay_screen_kernel(
                 y_block(2 * CHUNK, CHUNK, P, wq, (), 2)
 
         c, g = units[last]
-        z_first = weigh(sq[last], g, 0, P, SHARE_LAST)
+        z_first = weigh(z_tile(P)[:], sq[last], g, 0, P, SHARE_LAST)
         quantize_z(z[last - 1], *units[last - 1], 0, CHUNK)
         quantize_z(z_first, c, g, 0, P)
         y_block(c * CHUNK, P, P, wq, (), 4)
-        z_second = weigh(sq[last], g, P, P, 0)
+        z_second = weigh(z_tile(P)[:], sq[last], g, P, P, 0)
         quantize_z(z_second, c, g, P, P)
         y_block(c * CHUNK + P, P, P, wq, (0, 1), 2)

@@ -28,10 +28,11 @@ CHUNK = 256
 LOADED = 96
 PLANE_ROW = (0, 4)
 WN_STEP = 256
-SHARE = 64
+SHARE = 56
 SHARE_FROM = 3
 SHARE_LAST = 16
-JOINT = 1
+JOINT = 2
+TURN = 7
 AHEAD = 4
 
 
@@ -42,8 +43,7 @@ def tile_list_fragment_assay_screen_kernel(
     with ExitStack() as ctx:
         keep = ctx.enter_context(tc.tile_pool(name="keep", bufs=1))
         squares = ctx.enter_context(tc.tile_pool(name="squares", bufs=AHEAD + 1))
-        weighed = ctx.enter_context(tc.tile_pool(name="weighed", bufs=2))
-        psum = ctx.enter_context(tc.psum_pool(name="psum", bufs=7))
+        psum = ctx.enter_context(tc.psum_pool(name="psum", bufs=1))
         held = ctx.enter_context(tc.psum_pool(name="held", bufs=1))
 
         frag_list = keep.tile([P, S // STRIPE], U16, name="frag_list")
@@ -141,6 +141,12 @@ def tile_list_fragment_assay_screen_kernel(
         with nc.allow_non_contiguous_dma(reason="one bias value a partition"):
             nc.sync.dma_start(out=base_sb[:], in_=base.rearrange("(r p) -> p r", p=P))
 
+        taken = []
+
+        def bank_tile(shape):
+            taken.append(psum.tile(shape, F32, name="bank%d" % (len(taken) % TURN)))
+            return taken[-1]
+
         def a_pass(bank, a, c, g, t, joint):
             col = PASS * g + P * t
             nc.tensor.matmul_mx(
@@ -154,7 +160,7 @@ def tile_list_fragment_assay_screen_kernel(
             )
 
         def square_unit(c, g, joint=False):
-            banks = [psum.tile([P, 2, CHUNK], F32, name="bank") for u in range(2)]
+            banks = [bank_tile([P, 2, CHUNK]) for u in range(2)]
             for t in range(0, PACK, 1 if joint else 2):
                 a_pass(banks[t // 2], 0, c, g, t, joint)
             sq = squares.tile([P, 2, CHUNK, 2], F32, name="sq", align_bytes=64)
@@ -166,8 +172,8 @@ def tile_list_fragment_assay_screen_kernel(
                 nc.scalar.activation(sq[:, u], banks[u][:].rearrange("p e n -> p n e"), ACT.Square, bias=1.0)
             return sq
 
-        def z_tile(width):
-            return weighed.tile([P, width * PACK], BF16, name="z", align_bytes=64)
+        def z_tile(width, slot):
+            return keep.tile([P, width * PACK], BF16, name="z%d" % slot, align_bytes=64)
 
         def weigh(z, sq, g, lo, width, shared):
             own = width - shared
@@ -203,7 +209,7 @@ def tile_list_fragment_assay_screen_kernel(
             nc.vector.quantize_mx(out=codes[:].bitcast(FP8X4), scales=scales[:], in_=wn_il[:])
             return codes, scales
 
-        def y_pass(dst, g, r, h, cols, wq):
+        def y_pass(dst, g, r, h, cols, wq, start):
             if g == 0:
                 lhsT = w4[:, 2 * P * r : 2 * P * (r + 1)].bitcast(FP4X4)
                 lhsT_scale = w4_sc[:].bitcast(U8)[:, P * r : P * (r + 1)]
@@ -216,31 +222,45 @@ def tile_list_fragment_assay_screen_kernel(
                 lhsT_scale=lhsT_scale,
                 rhs=zq[h, g][0][:, cols].bitcast(FP8X4),
                 rhs_scale=zq[h, g][1][:, cols],
-                start=(g == 0),
-                stop=(g == 1),
+                start=start and g == 0,
+                stop=start and g == 1,
             )
 
         out_tiles = out.rearrange("(r p) j -> p r j", p=P)
 
-        def y_block(j0, width, group, wq, on_vector, per_store):
+        def y_open(j0, width, per_bank):
             h, off = divmod(j0, BANK)
-            banks = [psum.tile([P, width], F32, name="bank") for r in range(N // P)]
-            res = keep.tile([P, N // P, width], F32, name="res%d" % j0, align_bytes=64)
+            step = BANK if width == BANK else P
+            banks = [bank_tile([P, per_bank, width]) for b in range(N // P // per_bank)]
             for r in range(N // P):
-                y_pass(banks[r][:, :group], 0, r, h, slice(off, off + group), wq)
-            for r in range(N // P):
-                y_pass(banks[r][:, :group], 1, r, h, slice(off, off + group), wq)
-                for s in range(group, width, group):
-                    for g in range(2):
-                        y_pass(banks[r][:, s : s + group], g, r, h, slice(off + s, off + s + group), wq)
-                if r in on_vector:
-                    nc.vector.tensor_scalar(res[:, r, :], banks[r][:], base_sb[:, r : r + 1], None, ALU.add)
+                for s in range(0, width, step):
+                    dst = banks[r // per_bank][:, r % per_bank, s : s + step]
+                    y_pass(dst, 0, r, h, slice(off + s, off + s + step), None, r % per_bank == 0 and s == 0)
+            return j0, width, per_bank, banks
+
+        def y_sums(block, which, wq):
+            j0, width, per_bank, banks = block
+            h, off = divmod(j0, BANK)
+            for b in which:
+                for e in range(per_bank):
+                    y_pass(banks[b][:, e, :], 1, per_bank * b + e, h, slice(off, off + width), wq, e == per_bank - 1)
+
+        def y_leave(block, which, on_vector, queue, slot=None):
+            j0, width, per_bank, banks = block
+            r0, count = per_bank * which[0], per_bank * len(which)
+            res = keep.tile([P, count, width], F32, name=slot or "res%d_%d" % (j0, r0), align_bytes=64)
+            for i, b in enumerate(which):
+                rows = slice(per_bank * b, per_bank * (b + 1))
+                if on_vector:
+                    bias = base_sb[:, rows].unsqueeze(2).to_broadcast([P, per_bank, width])
+                    nc.vector.tensor_tensor(res[:, per_bank * i : per_bank * (i + 1), :], banks[b][:], bias, ALU.add)
                 else:
-                    nc.scalar.activation(res[:, r, :], banks[r][:], ACT.Identity, bias=base_sb[:, r : r + 1])
-                if (r + 1) % per_store == 0:
-                    rows = slice(r + 1 - per_store, r + 1)
-                    queue = nc.scalar if on_vector and r not in on_vector else nc.sync
-                    queue.dma_start(out=out_tiles[:, rows, j0 : j0 + width], in_=res[:, rows, :])
+                    for e in range(per_bank):
+                        r = rows.start + e
+                        nc.scalar.activation(
+                            res[:, r - r0, :], banks[b][:, e, :], ACT.Identity, bias=base_sb[:, r : r + 1]
+                        )
+            queue.dma_start(out=out_tiles[:, r0 : r0 + count, j0 : j0 + width], in_=res[:])
 
         units = [(c, g) for g in range(2) for c in range(2)] + [(c, g) for c in range(2, 4) for g in range(2)]
         last = len(units) - 1
@@ -253,28 +273,53 @@ def tile_list_fragment_assay_screen_kernel(
             cols = slice(n0, n0 + WN_STEP)
             nc.gpsimd.tensor_scalar(wn_dst[:, cols], wn_src[:, cols], 1.0, 0.0, ALU.mult, ALU.add)
 
-        pair = z_tile(2 * CHUNK)
-        z = []
-        for k in range(last):
-            dst = pair[:, PACK * CHUNK * k : PACK * CHUNK * (k + 1)] if k < 2 else z_tile(CHUNK)[:]
-            z.append(weigh(dst, sq[k], units[k][1], 0, CHUNK, SHARE if k >= SHARE_FROM else 0))
-            if k + AHEAD <= last:
-                sq.append(square_unit(*units[k + AHEAD]))
-            if k == 2:
-                quantize_z(pair[:], *units[0], 0, 2 * CHUNK)
-            if k > 2:
-                quantize_z(z[k - 1], *units[k - 1], 0, CHUNK)
-            if k == 4:
-                wq = quantize_wn(wn_il)
-                y_block(0, BANK, BANK, wq, (), 1)
-            if k == 6:
-                y_block(2 * CHUNK, CHUNK, P, wq, (), 2)
+        def weigh_unit(k, slot):
+            dst = z_tile(CHUNK, slot)[:]
+            return weigh(dst, sq[k], units[k][1], 0, CHUNK, SHARE if k >= SHARE_FROM else 0)
+
+        def quantize_unit(k):
+            quantize_z(z[k], *units[k], 0, CHUNK)
+
+        pair = z_tile(2 * CHUNK, 0)
+        z = {}
+        for k in range(2):
+            weigh(pair[:, PACK * CHUNK * k : PACK * CHUNK * (k + 1)], sq[k], units[k][1], 0, CHUNK, 0)
+            sq.append(square_unit(*units[k + AHEAD]))
+        z[2] = weigh_unit(2, 1)
+        sq.append(square_unit(*units[6]))
+        quantize_z(pair[:], *units[0], 0, 2 * CHUNK)
+        first = y_open(0, BANK, 1)
+        z[3] = weigh_unit(3, 0)
+        quantize_unit(2)
+        wq = quantize_wn(wn_il)
+        quantize_unit(3)
+        y_sums(first, (0, 1), wq)
+        y_leave(first, (0,), False, nc.sync)
+        sq.append(square_unit(*units[7]))
+        y_sums(first, (2, 3), wq)
+        z[4] = weigh_unit(4, 0)
+        for b in (1, 2, 3):
+            y_leave(first, (b,), False, nc.sync)
+        z[5] = weigh_unit(5, 1)
+        quantize_unit(4)
+        second = y_open(2 * CHUNK, CHUNK, 1)
+        z[6] = weigh_unit(6, 0)
+        quantize_unit(5)
+        y_sums(second, range(4), wq)
+        y_leave(second, (0, 1), False, nc.sync)
+        y_leave(second, (2, 3), False, nc.sync)
 
         c, g = units[last]
-        z_first = weigh(z_tile(P)[:], sq[last], g, 0, P, SHARE_LAST)
-        quantize_z(z[last - 1], *units[last - 1], 0, CHUNK)
+        z_first = weigh(z_tile(P, 1)[:], sq[last], g, 0, P, SHARE_LAST)
+        quantize_unit(last - 1)
+        third = y_open(c * CHUNK, P, 2)
+        fourth = y_open(c * CHUNK + P, P, 1)
         quantize_z(z_first, c, g, 0, P)
-        y_block(c * CHUNK, P, P, wq, (), 4)
-        z_second = weigh(z_tile(P)[:], sq[last], g, P, P, 0)
+        z_second = weigh(z_tile(P, 0)[:], sq[last], g, P, P, 0)
+        y_sums(third, range(2), wq)
+        y_leave(third, (0,), True, nc.sync)
+        y_leave(third, (1,), False, nc.sync)
         quantize_z(z_second, c, g, P, P)
-        y_block(c * CHUNK + P, P, P, wq, (0, 1), 2)
+        y_sums(fourth, (0, 2, 1, 3), wq)
+        y_leave(fourth, (0, 1), True, nc.sync)
+        y_leave(fourth, (2, 3), False, nc.scalar)

@@ -28,10 +28,10 @@ CHUNK = 256
 LOADED = 96
 PLANE_ROW = (0, 4)
 WN_STEP = 256
-SHARE = 56
+SHARE = 80
 SHARE_FROM = 3
-SHARE_LAST = 16
-JOINT = 2
+SHARE_LAST = 32
+JOINT = 1
 TURN = 7
 AHEAD = 4
 
@@ -42,7 +42,6 @@ def tile_list_fragment_assay_screen_kernel(
     nc = tc.nc
     with ExitStack() as ctx:
         keep = ctx.enter_context(tc.tile_pool(name="keep", bufs=1))
-        squares = ctx.enter_context(tc.tile_pool(name="squares", bufs=AHEAD + 1))
         psum = ctx.enter_context(tc.psum_pool(name="psum", bufs=1))
         held = ctx.enter_context(tc.psum_pool(name="held", bufs=1))
 
@@ -159,11 +158,12 @@ def tile_list_fragment_assay_screen_kernel(
                 stop=(a == 1 and not (joint and t % 2 == 0)),
             )
 
-        def square_unit(c, g, joint=False):
+        def square_unit(k, joint=False):
+            c, g = units[k]
             banks = [bank_tile([P, 2, CHUNK]) for u in range(2)]
             for t in range(0, PACK, 1 if joint else 2):
                 a_pass(banks[t // 2], 0, c, g, t, joint)
-            sq = squares.tile([P, 2, CHUNK, 2], F32, name="sq", align_bytes=64)
+            sq = keep.tile([P, 2, CHUNK, 2], F32, name="sq%d" % k, align_bytes=64)
             for u in range(2):
                 a_pass(banks[u], 1, c, g, 2 * u, joint)
                 if not joint:
@@ -173,7 +173,7 @@ def tile_list_fragment_assay_screen_kernel(
             return sq
 
         def z_tile(width, slot):
-            return keep.tile([P, width * PACK], BF16, name="z%d" % slot, align_bytes=64)
+            return keep.tile([P, width * PACK], BF16, name=slot, align_bytes=64)
 
         def weigh(z, sq, g, lo, width, shared):
             own = width - shared
@@ -264,7 +264,7 @@ def tile_list_fragment_assay_screen_kernel(
 
         units = [(c, g) for g in range(2) for c in range(2)] + [(c, g) for c in range(2, 4) for g in range(2)]
         last = len(units) - 1
-        sq = [square_unit(*units[k], joint=k < JOINT) for k in range(AHEAD)]
+        sq = [square_unit(k, joint=k < JOINT) for k in range(AHEAD)]
 
         wn_il = keep.tile([P, N * PACK], BF16, name="frag_sc_listed", align_bytes=64)
         wn_dst = wn_il[:].rearrange("p (n t) -> p n t", t=PACK)
@@ -280,45 +280,42 @@ def tile_list_fragment_assay_screen_kernel(
         def quantize_unit(k):
             quantize_z(z[k], *units[k], 0, CHUNK)
 
-        pair = z_tile(2 * CHUNK, 0)
+        pair = z_tile(2 * CHUNK, "z_pair")
         z = {}
         for k in range(2):
             weigh(pair[:, PACK * CHUNK * k : PACK * CHUNK * (k + 1)], sq[k], units[k][1], 0, CHUNK, 0)
-            sq.append(square_unit(*units[k + AHEAD]))
-        z[2] = weigh_unit(2, 1)
-        sq.append(square_unit(*units[6]))
+            sq.append(square_unit(k + AHEAD))
+        z[2] = weigh_unit(2, "z2")
+        sq.append(square_unit(6))
         quantize_z(pair[:], *units[0], 0, 2 * CHUNK)
-        first = y_open(0, BANK, 1)
-        z[3] = weigh_unit(3, 0)
+        z[3] = weigh_unit(3, "sq2")
+        sq.append(square_unit(7))
         quantize_unit(2)
         wq = quantize_wn(wn_il)
         quantize_unit(3)
-        y_sums(first, (0, 1), wq)
-        y_leave(first, (0,), False, nc.sync)
-        sq.append(square_unit(*units[7]))
-        y_sums(first, (2, 3), wq)
-        z[4] = weigh_unit(4, 0)
-        for b in (1, 2, 3):
+        first = y_open(0, BANK, 1)
+        y_sums(first, range(4), wq)
+        z[4] = weigh_unit(4, "frag_sc_listed")
+        for b in range(4):
             y_leave(first, (b,), False, nc.sync)
-        z[5] = weigh_unit(5, 1)
+        z[5] = weigh_unit(5, "sq2")
         quantize_unit(4)
         second = y_open(2 * CHUNK, CHUNK, 1)
-        z[6] = weigh_unit(6, 0)
+        z[6] = weigh_unit(6, "sq5")
         quantize_unit(5)
         y_sums(second, range(4), wq)
         y_leave(second, (0, 1), False, nc.sync)
         y_leave(second, (2, 3), False, nc.sync)
 
         c, g = units[last]
-        z_first = weigh(z_tile(P, 1)[:], sq[last], g, 0, P, SHARE_LAST)
+        z_first = weigh(z_tile(P, "sq6")[:], sq[last], g, 0, P, SHARE_LAST)
         quantize_unit(last - 1)
         third = y_open(c * CHUNK, P, 2)
         fourth = y_open(c * CHUNK + P, P, 1)
         quantize_z(z_first, c, g, 0, P)
-        z_second = weigh(z_tile(P, 0)[:], sq[last], g, P, P, 0)
+        z_second = weigh(z_tile(P, "z2")[:], sq[last], g, P, P, 0)
         y_sums(third, range(2), wq)
-        y_leave(third, (0,), True, nc.sync)
-        y_leave(third, (1,), False, nc.sync)
+        y_leave(third, (0, 1), False, nc.sync)
         quantize_z(z_second, c, g, P, P)
         y_sums(fourth, (0, 2, 1, 3), wq)
         y_leave(fourth, (0, 1), True, nc.sync)

@@ -26,7 +26,8 @@ ROWS = 4
 BANK = 512
 CHUNK = 256
 LOADED = 96
-PLANE_ROW = (0, 4)
+FRAG_ROW = (0, 4)
+ASSAY_ROW = (8, 4)
 WN_STEP = 256
 SHARE = 80
 SHARE_FROM = 3
@@ -47,7 +48,7 @@ def tile_list_fragment_assay_screen_kernel(
 
         frag_list = keep.tile([P, S // STRIPE], U16, name="frag_list")
         assay_list = keep.tile([P, S2 // STRIPE], U16, name="assay_list")
-        frag_tab = [keep.tile([P, T], I32, name="frag_tab%d" % a, align_bytes=64) for a in range(2)]
+        frag_tab = [keep.tile([P, T], I32, name="frag_tab0", align_bytes=64)]
         assay_tab = [keep.tile([P, T2], I32, name="assay_tab0", align_bytes=64)]
         frag_tab_sc = keep.tile([P, T // 4], I32, name="frag_tab_sc", align_bytes=64)
         assay_tab_sc = keep.tile([P, T2 // 4], I32, name="assay_tab_sc", align_bytes=64)
@@ -59,9 +60,10 @@ def tile_list_fragment_assay_screen_kernel(
         make_identity(nc, identity[:])
         nc.vector.memset(assay_tab_sc[:LOADED, :], 0)
         nc.vector.memset(frag_tab_sc[:LOADED, :], 0)
-        planes = [keep.tile([P, S + S2], U8, name="planes%d" % a, align_bytes=64) for a in range(2)]
-        for a in range(2):
-            nc.vector.memset(planes[a][:].bitcast(I32), 0)
+        assay_first = keep.tile([P, S2], U8, name="assay_first", align_bytes=64)
+        both_second = keep.tile([P, S + S2], U8, name="both_second", align_bytes=64)
+        for plane in (assay_first, both_second):
+            nc.vector.memset(plane[:].bitcast(I32), 0)
 
         def words(tab, a):
             return tab[a].rearrange("p t i -> p (t i)").bitcast(I32)
@@ -80,7 +82,6 @@ def tile_list_fragment_assay_screen_kernel(
         for t in range(PACK):
             nc.tensor.transpose(fw_ps[:, t:BANK:PACK], fw_rows[:, t:PASS:PACK], identity[:])
         nc.scalar.activation(fw_sb[:], fw_ps[:, : 2 * PACK], ACT.Identity)
-        nc.sync.dma_start(out=frag_tab[1][:], in_=words(tab_words, 1))
 
         frag = [[keep.tile([P, PASS], U32, name="frag%d%d" % (a, g), align_bytes=64) for g in range(2)] for a in range(2)]
         assay = [keep.tile([P, S2], U32, name="assay%d" % a, align_bytes=64) for a in range(2)]
@@ -89,6 +90,18 @@ def tile_list_fragment_assay_screen_kernel(
         staged = keep.tile([P, S + S2], U8, name="staged", align_bytes=64)
 
         nc.vector.tensor_copy(assay_sc_listed[:], assay_tab_sc[:].bitcast(U8).indirect(assay_list[:]))
+
+        def carry_scale_rows(plane, row, rows, a):
+            first = LOADED + 16 * a
+            for r in range(ROWS):
+                nc.sync.dma_start(
+                    out=plane[row + r : P : QUAD, :].bitcast(I32),
+                    in_=rows[first + r : first + 16 : ROWS].bitcast(I32),
+                )
+
+        carry_scale_rows(assay_first, ASSAY_ROW[0], assay_sc_listed[:], 0)
+        frag_tab.append(keep.tile([P, T], I32, name="assay_tab_sc", align_bytes=64))
+        nc.sync.dma_start(out=frag_tab[1][:], in_=words(tab_words, 1))
         nc.vector.tensor_copy(frag_sc_listed[:], frag_tab_sc[:].bitcast(U8).indirect(frag_list[:]))
         nc.vector.tensor_copy(staged[:, S:].bitcast(I32), assay_sc_listed[:].bitcast(I32))
         nc.vector.tensor_copy(
@@ -96,18 +109,13 @@ def tile_list_fragment_assay_screen_kernel(
             frag_sc_listed[:].rearrange("p (g m t) -> p g t m", g=2, t=PACK),
         )
 
-        def carry_scale_rows(a):
-            first = LOADED + 16 * a
-            for r in range(ROWS):
-                nc.sync.dma_start(
-                    out=planes[a][PLANE_ROW[a] + r : P : QUAD, :].bitcast(I32),
-                    in_=staged[first + r : first + 16 : ROWS, :].bitcast(I32),
-                )
-
-        carry_scale_rows(0)
+        frag_first = keep.tile([P, S], U8, name="frag_tab_sc", align_bytes=64)
+        carry_scale_rows(frag_first, FRAG_ROW[0], staged[:, :S], 0)
         assay_tab.append(keep.tile([P, T2], I32, name="frag_sc_listed", align_bytes=64))
         nc.sync.dma_start(out=assay_tab[1][:], in_=words(tab2_words, 1))
-        carry_scale_rows(1)
+        carry_scale_rows(both_second, FRAG_ROW[1], staged[:], 1)
+        frag_planes = (frag_first[FRAG_ROW[0] :, :], both_second[FRAG_ROW[1] :, :S])
+        assay_planes = (assay_first[ASSAY_ROW[0] :, :], both_second[ASSAY_ROW[1] :, S:])
 
         def gather_frag(a, g):
             nc.vector.tensor_copy(
@@ -129,8 +137,7 @@ def tile_list_fragment_assay_screen_kernel(
         nc.sync.dma_start(out=w4[:].bitcast(I32), in_=w4_words[0].bitcast(I32))
         gather_frag(1, 0)
         gather_frag(1, 1)
-        w4_sc = keep.tile([P, N // 4], I32, name="frag_tab1", align_bytes=64)
-        nc.gpsimd.memset(w4_sc[:], 0)
+        w4_sc = keep.tile([P, N // 4], I32, name="assay_tab_sc", align_bytes=64)
         for r in range(ROWS):
             nc.sync.dma_start(out=w4_sc[r:P:QUAD, :], in_=w4_scales[0, r:16:ROWS, :].bitcast(I32))
         gather_assay(1, 0, CHUNK)
@@ -151,9 +158,9 @@ def tile_list_fragment_assay_screen_kernel(
             nc.tensor.matmul_mx(
                 out=bank[:, t % 2, :],
                 lhsT=frag[a][g][:, P * t : P * t + P].bitcast(FP8X4),
-                lhsT_scale=planes[a][PLANE_ROW[a] :, col : col + P],
+                lhsT_scale=frag_planes[a][:, col : col + P],
                 rhs=assay[a][:, CHUNK * c : CHUNK * (c + 1)].bitcast(FP8X4),
-                rhs_scale=planes[a][PLANE_ROW[a] :, S + CHUNK * c : S + CHUNK * (c + 1)],
+                rhs_scale=assay_planes[a][:, CHUNK * c : CHUNK * (c + 1)],
                 start=(a == 0 and not (joint and t % 2 == 1)),
                 stop=(a == 1 and not (joint and t % 2 == 0)),
             )
@@ -293,8 +300,10 @@ def tile_list_fragment_assay_screen_kernel(
         quantize_unit(2)
         wq = quantize_wn(wn_il)
         quantize_unit(3)
-        first = y_open(0, BANK, 1)
-        y_sums(first, range(4), wq)
+        first = (0, BANK, 1, [bank_tile([P, 1, BANK]) for r in range(N // P)])
+        for r in range(N // P):
+            for e in range(2):
+                y_pass(first[3][r][:, 0, :], e, r, 0, slice(0, BANK), wq, True)
         z[4] = weigh_unit(4, "frag_sc_listed")
         for b in range(4):
             y_leave(first, (b,), False, nc.sync)

@@ -26,13 +26,13 @@ ROWS = 4
 BANK = 512
 CHUNK = 256
 LOADED = 96
-FRAG_ROW = (0, 4)
-ASSAY_ROW = (8, 4)
+KIB = 1024
+AT_FRAG0, AT_FRAG1, AT_ASSAY0, AT_FRAG_SC, AT_ONES = 0, 16, 32, 40, 45
 WN_STEP = 256
 SHARE = 80
 SHARE_FROM = 3
 SHARE_LAST = 32
-JOINT = 1
+JOINT = 2
 TURN = 7
 AHEAD = 4
 
@@ -46,12 +46,20 @@ def tile_list_fragment_assay_screen_kernel(
         psum = ctx.enter_context(tc.psum_pool(name="psum", bufs=1))
         held = ctx.enter_context(tc.psum_pool(name="held", bufs=1))
 
+        laid = ctx.enter_context(tc.tile_pool(name="laid", bufs=1))
+
+        def tile(shape, dtype, name):
+            return keep.tile(shape, dtype, name=name, align_bytes=64)
+
+        def placed(shape, dtype, name, kib):
+            return laid.tile(shape, dtype, name=name, align_bytes=64, offset=kib * KIB)
+
         frag_list = keep.tile([P, S // STRIPE], U16, name="frag_list")
         assay_list = keep.tile([P, S2 // STRIPE], U16, name="assay_list")
-        frag_tab = [keep.tile([P, T], I32, name="frag_tab0", align_bytes=64)]
-        assay_tab = [keep.tile([P, T2], I32, name="assay_tab0", align_bytes=64)]
-        frag_tab_sc = keep.tile([P, T // 4], I32, name="frag_tab_sc", align_bytes=64)
-        assay_tab_sc = keep.tile([P, T2 // 4], I32, name="assay_tab_sc", align_bytes=64)
+        frag_tab = [placed([P, T], I32, "frag_tab0", AT_FRAG0)]
+        assay_tab = [placed([P, T2], I32, "assay_tab0", AT_ASSAY0)]
+        frag_tab_sc = placed([P, T // 4], I32, "frag_tab_sc", AT_FRAG_SC)
+        assay_tab_sc = placed([P, T2 // 4], I32, "assay_tab_sc", AT_FRAG1)
         fw_rows = keep.tile([P, PASS], F32, name="fw_rows")
         fw_sb = keep.tile([P, 2 * PACK], F32, name="fw_sb")
         identity = keep.tile([P, P], F32, name="identity")
@@ -60,10 +68,10 @@ def tile_list_fragment_assay_screen_kernel(
         make_identity(nc, identity[:])
         nc.vector.memset(assay_tab_sc[:LOADED, :], 0)
         nc.vector.memset(frag_tab_sc[:LOADED, :], 0)
-        assay_first = keep.tile([P, S2], U8, name="assay_first", align_bytes=64)
-        both_second = keep.tile([P, S + S2], U8, name="both_second", align_bytes=64)
-        for plane in (assay_first, both_second):
-            nc.vector.memset(plane[:].bitcast(I32), 0)
+
+        ones = {k: laid.tile([P, 16], F32, name="one%d" % k, offset=at * KIB - 32) for k, at in ((2, AT_ONES), (3, AT_ONES + 1))}
+        for one in ones.values():
+            nc.gpsimd.memset(one[:, :1], 1.0)
 
         def words(tab, a):
             return tab[a].rearrange("p t i -> p (t i)").bitcast(I32)
@@ -83,39 +91,38 @@ def tile_list_fragment_assay_screen_kernel(
             nc.tensor.transpose(fw_ps[:, t:BANK:PACK], fw_rows[:, t:PASS:PACK], identity[:])
         nc.scalar.activation(fw_sb[:], fw_ps[:, : 2 * PACK], ACT.Identity)
 
-        frag = [[keep.tile([P, PASS], U32, name="frag%d%d" % (a, g), align_bytes=64) for g in range(2)] for a in range(2)]
-        assay = [keep.tile([P, S2], U32, name="assay%d" % a, align_bytes=64) for a in range(2)]
-        frag_sc_listed = keep.tile([P, S], U8, name="frag_sc_listed", align_bytes=64)
-        assay_sc_listed = keep.tile([P, S2], U8, name="assay_sc_listed", align_bytes=64)
-        staged = keep.tile([P, S + S2], U8, name="staged", align_bytes=64)
+        frag = [[tile([P, PASS], U32, "frag%d%d" % (a, g)) for g in range(2)] for a in range(2)]
+        assay = [tile([P, S2], U32, "assay%d" % a) for a in range(2)]
+        frag_sc_listed = tile([P, S], U8, "frag_sc_listed")
+        assay_sc_listed = tile([P, S2], U8, "assay_sc_listed")
+        staged = tile([P, 2, 2, PASS], U8, "staged")
 
         nc.vector.tensor_copy(assay_sc_listed[:], assay_tab_sc[:].bitcast(U8).indirect(assay_list[:]))
+        frag_tab.append(placed([P, T], I32, "frag_tab1", AT_FRAG1))
+        nc.sync.dma_start(out=frag_tab[1][:], in_=words(tab_words, 1))
+        nc.vector.tensor_copy(frag_sc_listed[:], frag_tab_sc[:].bitcast(U8).indirect(frag_list[:]))
+        nc.vector.tensor_copy(
+            staged[:, :, 1, :].bitcast(I32), assay_sc_listed[:].bitcast(I32).rearrange("p (h n) -> p h n", h=2)
+        )
+        nc.vector.tensor_copy(
+            staged[:, :, 0, :].rearrange("p g (t m) -> p g t m", t=PACK),
+            frag_sc_listed[:].rearrange("p (g m t) -> p g t m", g=2, t=PACK),
+        )
+        staged_rows = staged[:].rearrange("p h s n -> p (h s n)")
 
-        def carry_scale_rows(plane, row, rows, a):
+        def carry_scale_rows(plane, row, a, lo, hi):
             first = LOADED + 16 * a
             for r in range(ROWS):
                 nc.sync.dma_start(
                     out=plane[row + r : P : QUAD, :].bitcast(I32),
-                    in_=rows[first + r : first + 16 : ROWS].bitcast(I32),
+                    in_=staged_rows[first + r : first + 16 : ROWS, lo:hi].bitcast(I32),
                 )
+            return plane[row:, :]
 
-        carry_scale_rows(assay_first, ASSAY_ROW[0], assay_sc_listed[:], 0)
-        frag_tab.append(keep.tile([P, T], I32, name="assay_tab_sc", align_bytes=64))
-        nc.sync.dma_start(out=frag_tab[1][:], in_=words(tab_words, 1))
-        nc.vector.tensor_copy(frag_sc_listed[:], frag_tab_sc[:].bitcast(U8).indirect(frag_list[:]))
-        nc.vector.tensor_copy(staged[:, S:].bitcast(I32), assay_sc_listed[:].bitcast(I32))
-        nc.vector.tensor_copy(
-            staged[:, :S].rearrange("p (g t m) -> p g t m", g=2, t=PACK),
-            frag_sc_listed[:].rearrange("p (g m t) -> p g t m", g=2, t=PACK),
-        )
-
-        frag_first = keep.tile([P, S], U8, name="frag_tab_sc", align_bytes=64)
-        carry_scale_rows(frag_first, FRAG_ROW[0], staged[:, :S], 0)
-        assay_tab.append(keep.tile([P, T2], I32, name="frag_sc_listed", align_bytes=64))
+        early = carry_scale_rows(placed([P, 2 * PASS], U8, "early", AT_FRAG_SC), 0, 0, 0, 2 * PASS)
+        assay_tab.append(tile([P, T2], I32, "frag_sc_listed"))
         nc.sync.dma_start(out=assay_tab[1][:], in_=words(tab2_words, 1))
-        carry_scale_rows(both_second, FRAG_ROW[1], staged[:], 1)
-        frag_planes = (frag_first[FRAG_ROW[0] :, :], both_second[FRAG_ROW[1] :, :S])
-        assay_planes = (assay_first[ASSAY_ROW[0] :, :], both_second[ASSAY_ROW[1] :, S:])
+        second = carry_scale_rows(placed([P, 4 * PASS], U8, "second", AT_FRAG_SC + 1), 4, 1, 0, 4 * PASS)
 
         def gather_frag(a, g):
             nc.vector.tensor_copy(
@@ -128,24 +135,29 @@ def tile_list_fragment_assay_screen_kernel(
                 assay[a][:, lo:hi], assay_tab[a][:].bitcast(U32).indirect(assay_list[:, lo // STRIPE : hi // STRIPE])
             )
 
+        wn_rows = wn.rearrange("(p t) n -> p t n", t=PACK)
         gather_assay(0, 0, S2)
-        wn_raw = keep.tile([P, PACK, N], F32, name="assay_tab0", align_bytes=64)
-        nc.sync.dma_start(out=wn_raw[:], in_=wn.rearrange("(p t) n -> p t n", t=PACK))
+        wn_raw = [placed([P, PACK, WN_STEP], F32, "wn_raw0", AT_ASSAY0)]
+        nc.sync.dma_start(out=wn_raw[0][:], in_=wn_rows[:, :, :WN_STEP])
         gather_frag(0, 0)
         gather_frag(0, 1)
-        w4 = keep.tile([P, 2 * N], U8, name="frag_tab0", align_bytes=64)
-        nc.sync.dma_start(out=w4[:].bitcast(I32), in_=w4_words[0].bitcast(I32))
+        late = carry_scale_rows(placed([P, 2 * PASS], U8, "late", AT_FRAG0), 8, 0, 2 * PASS, 4 * PASS)
+        planes = ((early, late), (second[:, : 2 * PASS], second[:, 2 * PASS :]))
         gather_frag(1, 0)
         gather_frag(1, 1)
-        w4_sc = keep.tile([P, N // 4], I32, name="assay_tab_sc", align_bytes=64)
+        wn_raw.append(placed([P, PACK, WN_STEP], F32, "wn_raw1", AT_FRAG1))
+        nc.sync.dma_start(out=wn_raw[1][:], in_=wn_rows[:, :, WN_STEP:])
+        w4 = placed([P, 2 * N], U8, "w4", AT_FRAG1 + 4)
+        nc.sync.dma_start(out=w4[:].bitcast(I32), in_=w4_words[0].bitcast(I32))
+        w4_sc = placed([P, N // 4], I32, "w4_sc", AT_FRAG1 + 5)
         for r in range(ROWS):
             nc.sync.dma_start(out=w4_sc[r:P:QUAD, :], in_=w4_scales[0, r:16:ROWS, :].bitcast(I32))
+        base_sb = placed([P, N // P], F32, "base_sb", AT_FRAG1 + 6)
+        with nc.allow_non_contiguous_dma(reason="one bias value a partition"):
+            nc.sync.dma_start(out=base_sb[:], in_=base.rearrange("(r p) -> p r", p=P))
         gather_assay(1, 0, CHUNK)
         gather_assay(1, CHUNK, 2 * CHUNK)
         gather_assay(1, 2 * CHUNK, S2)
-        base_sb = keep.tile([P, N // P], F32, name="staged", align_bytes=64)
-        with nc.allow_non_contiguous_dma(reason="one bias value a partition"):
-            nc.sync.dma_start(out=base_sb[:], in_=base.rearrange("(r p) -> p r", p=P))
 
         taken = []
 
@@ -154,13 +166,13 @@ def tile_list_fragment_assay_screen_kernel(
             return taken[-1]
 
         def a_pass(bank, a, c, g, t, joint):
-            col = PASS * g + P * t
+            col = PASS + CHUNK * (c % 2)
             nc.tensor.matmul_mx(
                 out=bank[:, t % 2, :],
                 lhsT=frag[a][g][:, P * t : P * t + P].bitcast(FP8X4),
-                lhsT_scale=frag_planes[a][:, col : col + P],
+                lhsT_scale=planes[a][g][:, P * t : P * t + P],
                 rhs=assay[a][:, CHUNK * c : CHUNK * (c + 1)].bitcast(FP8X4),
-                rhs_scale=assay_planes[a][:, CHUNK * c : CHUNK * (c + 1)],
+                rhs_scale=planes[a][c // 2][:, col : col + CHUNK],
                 start=(a == 0 and not (joint and t % 2 == 1)),
                 stop=(a == 1 and not (joint and t % 2 == 0)),
             )
@@ -170,16 +182,20 @@ def tile_list_fragment_assay_screen_kernel(
             banks = [bank_tile([P, 2, CHUNK]) for u in range(2)]
             for t in range(0, PACK, 1 if joint else 2):
                 a_pass(banks[t // 2], 0, c, g, t, joint)
-            sq = keep.tile([P, 2, CHUNK, 2], F32, name="sq%d" % k, align_bytes=64)
+            shape = [P, 2, CHUNK, 2]
+            sq = placed(shape, F32, "sq2", AT_FRAG1 - 4) if k == 2 else tile(shape, F32, "sq%d" % k)
             for u in range(2):
                 a_pass(banks[u], 1, c, g, 2 * u, joint)
                 if not joint:
                     a_pass(banks[u], 0, c, g, 2 * u + 1, joint)
                 a_pass(banks[u], 1, c, g, 2 * u + 1, joint)
-                nc.scalar.activation(sq[:, u], banks[u][:].rearrange("p e n -> p n e"), ACT.Square, bias=1.0)
+                one = ones[k][:, :1] if k in ones else 1.0
+                nc.scalar.activation(sq[:, u], banks[u][:].rearrange("p e n -> p n e"), ACT.Square, bias=one)
             return sq
 
         def z_tile(width, slot):
+            if slot in ("z3", "z5"):
+                return placed([P, width * PACK], BF16, slot, AT_FRAG1 - 1)
             return keep.tile([P, width * PACK], BF16, name=slot, align_bytes=64)
 
         def weigh(z, sq, g, lo, width, shared):
@@ -202,7 +218,9 @@ def tile_list_fragment_assay_screen_kernel(
             for g in range(2):
                 zq[h, g] = (
                     keep.tile([P, BANK], U32, name="z_codes%d%d" % (h, g), align_bytes=64),
-                    keep.tile([P, BANK], U8, name="z_scales%d%d" % (h, g), align_bytes=64),
+                    laid.tile([P, BANK], U8, name="z_scales0%d" % g, align_bytes=64, offset=(AT_ONES + g) * KIB - BANK)
+                    if h == 0
+                    else tile([P, BANK], U8, "z_scales1%d" % g),
                 )
 
         def quantize_z(z, c, g, lo, width):
@@ -212,7 +230,7 @@ def tile_list_fragment_assay_screen_kernel(
 
         def quantize_wn(wn_il):
             codes = keep.tile([P, N], U32, name="wn_codes", align_bytes=64)
-            scales = keep.tile([P, N], U8, name="wn_scales", align_bytes=64)
+            scales = placed([P, N], U8, "wn_scales", AT_ONES + 1)
             nc.vector.quantize_mx(out=codes[:].bitcast(FP8X4), scales=scales[:], in_=wn_il[:])
             return codes, scales
 
@@ -275,10 +293,9 @@ def tile_list_fragment_assay_screen_kernel(
 
         wn_il = keep.tile([P, N * PACK], BF16, name="frag_sc_listed", align_bytes=64)
         wn_dst = wn_il[:].rearrange("p (n t) -> p n t", t=PACK)
-        wn_src = wn_raw[:].rearrange("p t n -> p n t")
-        for n0 in range(0, N, WN_STEP):
-            cols = slice(n0, n0 + WN_STEP)
-            nc.gpsimd.tensor_scalar(wn_dst[:, cols], wn_src[:, cols], 1.0, 0.0, ALU.mult, ALU.add)
+        for h in range(2):
+            cols = slice(WN_STEP * h, WN_STEP * (h + 1))
+            nc.gpsimd.tensor_scalar(wn_dst[:, cols], wn_raw[h][:].rearrange("p t n -> p n t"), 1.0, 0.0, ALU.mult, ALU.add)
 
         def weigh_unit(k, slot):
             dst = z_tile(CHUNK, slot)[:]
@@ -295,7 +312,7 @@ def tile_list_fragment_assay_screen_kernel(
         z[2] = weigh_unit(2, "z2")
         sq.append(square_unit(6))
         quantize_z(pair[:], *units[0], 0, 2 * CHUNK)
-        z[3] = weigh_unit(3, "sq2")
+        z[3] = weigh_unit(3, "z3")
         sq.append(square_unit(7))
         quantize_unit(2)
         wq = quantize_wn(wn_il)
@@ -307,7 +324,7 @@ def tile_list_fragment_assay_screen_kernel(
         z[4] = weigh_unit(4, "frag_sc_listed")
         for b in range(4):
             y_leave(first, (b,), False, nc.sync)
-        z[5] = weigh_unit(5, "sq2")
+        z[5] = weigh_unit(5, "z5")
         quantize_unit(4)
         second = y_open(2 * CHUNK, CHUNK, 1)
         z[6] = weigh_unit(6, "sq5")

@@ -32,7 +32,7 @@ WN_STEP = 256
 SHARE = 80
 SHARE_FROM = 3
 SHARE_LAST = 32
-JOINT = 2
+JOINT = 1
 TURN = 7
 AHEAD = 4
 
@@ -59,7 +59,7 @@ def tile_list_fragment_assay_screen_kernel(
         frag_tab = [placed([P, T], I32, "frag_tab0", AT_FRAG0)]
         assay_tab = [placed([P, T2], I32, "assay_tab0", AT_ASSAY0)]
         frag_tab_sc = placed([P, T // 4], I32, "frag_tab_sc", AT_FRAG_SC)
-        assay_tab_sc = placed([P, T2 // 4], I32, "assay_tab_sc", AT_FRAG1)
+        assay_tab_sc = tile([P, T2 // 4], I32, "assay_tab_sc")
         fw_rows = keep.tile([P, PASS], F32, name="fw_rows")
         fw_sb = keep.tile([P, 2 * PACK], F32, name="fw_sb")
         identity = keep.tile([P, P], F32, name="identity")
@@ -82,7 +82,6 @@ def tile_list_fragment_assay_screen_kernel(
         ):
             nc.sync.dma_start(listed[:], entries)
             nc.sync.dma_start(out=window[LOADED:, :], in_=rows.rearrange("a q t -> (a q) t").bitcast(I32))
-        nc.sync.dma_start(out=assay_tab[0][:], in_=words(tab2_words, 0))
         nc.sync.dma_start(out=frag_tab[0][:], in_=words(tab_words, 0))
 
         nc.sync.dma_start(out=fw_rows[0:2, :], in_=fw.rearrange("(g i) -> g i", g=2))
@@ -90,39 +89,37 @@ def tile_list_fragment_assay_screen_kernel(
         for t in range(PACK):
             nc.tensor.transpose(fw_ps[:, t:BANK:PACK], fw_rows[:, t:PASS:PACK], identity[:])
         nc.scalar.activation(fw_sb[:], fw_ps[:, : 2 * PACK], ACT.Identity)
+        frag_tab.append(placed([P, T], I32, "frag_tab1", AT_FRAG1))
+        nc.sync.dma_start(out=frag_tab[1][:], in_=words(tab_words, 1))
+        nc.sync.dma_start(out=assay_tab[0][:], in_=words(tab2_words, 0))
 
         frag = [[tile([P, PASS], U32, "frag%d%d" % (a, g)) for g in range(2)] for a in range(2)]
         assay = [tile([P, S2], U32, "assay%d" % a) for a in range(2)]
         frag_sc_listed = tile([P, S], U8, "frag_sc_listed")
         assay_sc_listed = tile([P, S2], U8, "assay_sc_listed")
-        staged = tile([P, 2, 2, PASS], U8, "staged")
+        staged = tile([P, S + S2], U8, "staged")
 
         nc.vector.tensor_copy(assay_sc_listed[:], assay_tab_sc[:].bitcast(U8).indirect(assay_list[:]))
-        frag_tab.append(placed([P, T], I32, "frag_tab1", AT_FRAG1))
-        nc.sync.dma_start(out=frag_tab[1][:], in_=words(tab_words, 1))
         nc.vector.tensor_copy(frag_sc_listed[:], frag_tab_sc[:].bitcast(U8).indirect(frag_list[:]))
+        nc.vector.tensor_copy(staged[:, S:].bitcast(I32), assay_sc_listed[:].bitcast(I32))
         nc.vector.tensor_copy(
-            staged[:, :, 1, :].bitcast(I32), assay_sc_listed[:].bitcast(I32).rearrange("p (h n) -> p h n", h=2)
-        )
-        nc.vector.tensor_copy(
-            staged[:, :, 0, :].rearrange("p g (t m) -> p g t m", t=PACK),
+            staged[:, :S].rearrange("p (g t m) -> p g t m", g=2, t=PACK),
             frag_sc_listed[:].rearrange("p (g m t) -> p g t m", g=2, t=PACK),
         )
-        staged_rows = staged[:].rearrange("p h s n -> p (h s n)")
 
-        def carry_scale_rows(plane, row, a, lo, hi):
+        def carry_scale_rows(plane, a):
             first = LOADED + 16 * a
             for r in range(ROWS):
                 nc.sync.dma_start(
-                    out=plane[row + r : P : QUAD, :].bitcast(I32),
-                    in_=staged_rows[first + r : first + 16 : ROWS, lo:hi].bitcast(I32),
+                    out=plane[ROWS * a + r : P : QUAD, :].bitcast(I32),
+                    in_=staged[first + r : first + 16 : ROWS].bitcast(I32),
                 )
-            return plane[row:, :]
+            return plane[ROWS * a :, :]
 
-        early = carry_scale_rows(placed([P, 2 * PASS], U8, "early", AT_FRAG_SC), 0, 0, 0, 2 * PASS)
+        planes = [carry_scale_rows(placed([P, S + S2], U8, "plane0", AT_FRAG_SC), 0)]
         assay_tab.append(tile([P, T2], I32, "frag_sc_listed"))
         nc.sync.dma_start(out=assay_tab[1][:], in_=words(tab2_words, 1))
-        second = carry_scale_rows(placed([P, 4 * PASS], U8, "second", AT_FRAG_SC + 1), 4, 1, 0, 4 * PASS)
+        planes.append(carry_scale_rows(placed([P, S + S2], U8, "plane1", AT_FRAG_SC + 2), 1))
 
         def gather_frag(a, g):
             nc.vector.tensor_copy(
@@ -130,23 +127,19 @@ def tile_list_fragment_assay_screen_kernel(
                 frag_tab[a][:].bitcast(U32).indirect(frag_list[:, PASS * g // STRIPE : PASS * (g + 1) // STRIPE]),
             )
 
-        def gather_assay(a, lo, hi):
-            nc.vector.tensor_copy(
-                assay[a][:, lo:hi], assay_tab[a][:].bitcast(U32).indirect(assay_list[:, lo // STRIPE : hi // STRIPE])
-            )
+        def gather_assay(a):
+            for lo, hi in ((0, CHUNK), (CHUNK, 2 * CHUNK), (2 * CHUNK, S2)):
+                nc.vector.tensor_copy(
+                    assay[a][:, lo:hi],
+                    assay_tab[a][:].bitcast(U32).indirect(assay_list[:, lo // STRIPE : hi // STRIPE]),
+                )
 
-        wn_rows = wn.rearrange("(p t) n -> p t n", t=PACK)
-        gather_assay(0, 0, S2)
-        wn_raw = [placed([P, PACK, WN_STEP], F32, "wn_raw0", AT_ASSAY0)]
-        nc.sync.dma_start(out=wn_raw[0][:], in_=wn_rows[:, :, :WN_STEP])
         gather_frag(0, 0)
         gather_frag(0, 1)
-        late = carry_scale_rows(placed([P, 2 * PASS], U8, "late", AT_FRAG0), 8, 0, 2 * PASS, 4 * PASS)
-        planes = ((early, late), (second[:, : 2 * PASS], second[:, 2 * PASS :]))
+        wn_raw = placed([P, PACK, N], F32, "wn_raw", AT_FRAG0)
+        nc.sync.dma_start(out=wn_raw[:], in_=wn.rearrange("(p t) n -> p t n", t=PACK))
         gather_frag(1, 0)
         gather_frag(1, 1)
-        wn_raw.append(placed([P, PACK, WN_STEP], F32, "wn_raw1", AT_FRAG1))
-        nc.sync.dma_start(out=wn_raw[1][:], in_=wn_rows[:, :, WN_STEP:])
         w4 = placed([P, 2 * N], U8, "w4", AT_FRAG1 + 4)
         nc.sync.dma_start(out=w4[:].bitcast(I32), in_=w4_words[0].bitcast(I32))
         w4_sc = placed([P, N // 4], I32, "w4_sc", AT_FRAG1 + 5)
@@ -155,9 +148,8 @@ def tile_list_fragment_assay_screen_kernel(
         base_sb = placed([P, N // P], F32, "base_sb", AT_FRAG1 + 6)
         with nc.allow_non_contiguous_dma(reason="one bias value a partition"):
             nc.sync.dma_start(out=base_sb[:], in_=base.rearrange("(r p) -> p r", p=P))
-        gather_assay(1, 0, CHUNK)
-        gather_assay(1, CHUNK, 2 * CHUNK)
-        gather_assay(1, 2 * CHUNK, S2)
+        gather_assay(0)
+        gather_assay(1)
 
         taken = []
 
@@ -166,13 +158,13 @@ def tile_list_fragment_assay_screen_kernel(
             return taken[-1]
 
         def a_pass(bank, a, c, g, t, joint):
-            col = PASS + CHUNK * (c % 2)
+            col = PASS * g + P * t
             nc.tensor.matmul_mx(
                 out=bank[:, t % 2, :],
                 lhsT=frag[a][g][:, P * t : P * t + P].bitcast(FP8X4),
-                lhsT_scale=planes[a][g][:, P * t : P * t + P],
+                lhsT_scale=planes[a][:, col : col + P],
                 rhs=assay[a][:, CHUNK * c : CHUNK * (c + 1)].bitcast(FP8X4),
-                rhs_scale=planes[a][c // 2][:, col : col + CHUNK],
+                rhs_scale=planes[a][:, S + CHUNK * c : S + CHUNK * (c + 1)],
                 start=(a == 0 and not (joint and t % 2 == 1)),
                 stop=(a == 1 and not (joint and t % 2 == 0)),
             )
@@ -182,8 +174,7 @@ def tile_list_fragment_assay_screen_kernel(
             banks = [bank_tile([P, 2, CHUNK]) for u in range(2)]
             for t in range(0, PACK, 1 if joint else 2):
                 a_pass(banks[t // 2], 0, c, g, t, joint)
-            shape = [P, 2, CHUNK, 2]
-            sq = placed(shape, F32, "sq2", AT_FRAG1 - 4) if k == 2 else tile(shape, F32, "sq%d" % k)
+            sq = tile([P, 2, CHUNK, 2], F32, "sq%d" % k)
             for u in range(2):
                 a_pass(banks[u], 1, c, g, 2 * u, joint)
                 if not joint:
@@ -194,8 +185,6 @@ def tile_list_fragment_assay_screen_kernel(
             return sq
 
         def z_tile(width, slot):
-            if slot in ("z3", "z5"):
-                return placed([P, width * PACK], BF16, slot, AT_FRAG1 - 1)
             return keep.tile([P, width * PACK], BF16, name=slot, align_bytes=64)
 
         def weigh(z, sq, g, lo, width, shared):
@@ -293,9 +282,10 @@ def tile_list_fragment_assay_screen_kernel(
 
         wn_il = keep.tile([P, N * PACK], BF16, name="frag_sc_listed", align_bytes=64)
         wn_dst = wn_il[:].rearrange("p (n t) -> p n t", t=PACK)
-        for h in range(2):
-            cols = slice(WN_STEP * h, WN_STEP * (h + 1))
-            nc.gpsimd.tensor_scalar(wn_dst[:, cols], wn_raw[h][:].rearrange("p t n -> p n t"), 1.0, 0.0, ALU.mult, ALU.add)
+        wn_src = wn_raw[:].rearrange("p t n -> p n t")
+        for n0 in range(0, N, WN_STEP):
+            cols = slice(n0, n0 + WN_STEP)
+            nc.gpsimd.tensor_scalar(wn_dst[:, cols], wn_src[:, cols], 1.0, 0.0, ALU.mult, ALU.add)
 
         def weigh_unit(k, slot):
             dst = z_tile(CHUNK, slot)[:]
@@ -312,7 +302,7 @@ def tile_list_fragment_assay_screen_kernel(
         z[2] = weigh_unit(2, "z2")
         sq.append(square_unit(6))
         quantize_z(pair[:], *units[0], 0, 2 * CHUNK)
-        z[3] = weigh_unit(3, "z3")
+        z[3] = weigh_unit(3, "sq2")
         sq.append(square_unit(7))
         quantize_unit(2)
         wq = quantize_wn(wn_il)
@@ -324,7 +314,7 @@ def tile_list_fragment_assay_screen_kernel(
         z[4] = weigh_unit(4, "frag_sc_listed")
         for b in range(4):
             y_leave(first, (b,), False, nc.sync)
-        z[5] = weigh_unit(5, "z5")
+        z[5] = weigh_unit(5, "sq2")
         quantize_unit(4)
         second = y_open(2 * CHUNK, CHUNK, 1)
         z[6] = weigh_unit(6, "sq5")

@@ -27,7 +27,7 @@ BANK = 512
 CHUNK = 256
 LOADED = 96
 KIB = 1024
-AT_FRAG0, AT_FRAG1, AT_ASSAY0, AT_FRAG_SC, AT_ONES = 0, 16, 32, 40, 45
+AT_FRAG0, AT_FRAG1, AT_ASSAY0, AT_FRAG_SC, AT_ONES = 0, 17, 34, 42, 47
 WN_STEP = 256
 SHARE = 80
 SHARE_FROM = 3
@@ -59,7 +59,7 @@ def tile_list_fragment_assay_screen_kernel(
         frag_tab = [placed([P, T], I32, "frag_tab0", AT_FRAG0)]
         assay_tab = [placed([P, T2], I32, "assay_tab0", AT_ASSAY0)]
         frag_tab_sc = placed([P, T // 4], I32, "frag_tab_sc", AT_FRAG_SC)
-        assay_tab_sc = tile([P, T2 // 4], I32, "assay_tab_sc")
+        assay_tab_sc = placed([P, T2 // 4], I32, "assay_tab_sc", AT_FRAG1 - 1)
         fw_rows = keep.tile([P, PASS], F32, name="fw_rows")
         fw_sb = keep.tile([P, 2 * PACK], F32, name="fw_sb")
         identity = keep.tile([P, P], F32, name="identity")
@@ -82,6 +82,7 @@ def tile_list_fragment_assay_screen_kernel(
         ):
             nc.sync.dma_start(listed[:], entries)
             nc.sync.dma_start(out=window[LOADED:, :], in_=rows.rearrange("a q t -> (a q) t").bitcast(I32))
+        nc.sync.dma_start(out=assay_tab[0][:], in_=words(tab2_words, 0))
         nc.sync.dma_start(out=frag_tab[0][:], in_=words(tab_words, 0))
 
         nc.sync.dma_start(out=fw_rows[0:2, :], in_=fw.rearrange("(g i) -> g i", g=2))
@@ -89,9 +90,6 @@ def tile_list_fragment_assay_screen_kernel(
         for t in range(PACK):
             nc.tensor.transpose(fw_ps[:, t:BANK:PACK], fw_rows[:, t:PASS:PACK], identity[:])
         nc.scalar.activation(fw_sb[:], fw_ps[:, : 2 * PACK], ACT.Identity)
-        frag_tab.append(placed([P, T], I32, "frag_tab1", AT_FRAG1))
-        nc.sync.dma_start(out=frag_tab[1][:], in_=words(tab_words, 1))
-        nc.sync.dma_start(out=assay_tab[0][:], in_=words(tab2_words, 0))
 
         frag = [[tile([P, PASS], U32, "frag%d%d" % (a, g)) for g in range(2)] for a in range(2)]
         assay = [tile([P, S2], U32, "assay%d" % a) for a in range(2)]
@@ -99,27 +97,31 @@ def tile_list_fragment_assay_screen_kernel(
         assay_sc_listed = tile([P, S2], U8, "assay_sc_listed")
         staged = tile([P, S + S2], U8, "staged")
 
+        def carry_scale_rows(plane, row, rows, a):
+            first = LOADED + 16 * a
+            for r in range(ROWS):
+                nc.sync.dma_start(
+                    out=plane[row + r : P : QUAD, :].bitcast(I32),
+                    in_=rows[first + r : first + 16 : ROWS].bitcast(I32),
+                )
+            return plane[row:, :]
+
         nc.vector.tensor_copy(assay_sc_listed[:], assay_tab_sc[:].bitcast(U8).indirect(assay_list[:]))
+        assay_first = carry_scale_rows(placed([P, S2], U8, "assay_first", AT_FRAG1 - 1), 8, assay_sc_listed[:], 0)
+        frag_tab.append(placed([P, T], I32, "frag_tab1", AT_FRAG1))
+        nc.sync.dma_start(out=frag_tab[1][:], in_=words(tab_words, 1))
         nc.vector.tensor_copy(frag_sc_listed[:], frag_tab_sc[:].bitcast(U8).indirect(frag_list[:]))
         nc.vector.tensor_copy(staged[:, S:].bitcast(I32), assay_sc_listed[:].bitcast(I32))
         nc.vector.tensor_copy(
             staged[:, :S].rearrange("p (g t m) -> p g t m", g=2, t=PACK),
             frag_sc_listed[:].rearrange("p (g m t) -> p g t m", g=2, t=PACK),
         )
-
-        def carry_scale_rows(plane, a):
-            first = LOADED + 16 * a
-            for r in range(ROWS):
-                nc.sync.dma_start(
-                    out=plane[ROWS * a + r : P : QUAD, :].bitcast(I32),
-                    in_=staged[first + r : first + 16 : ROWS].bitcast(I32),
-                )
-            return plane[ROWS * a :, :]
-
-        planes = [carry_scale_rows(placed([P, S + S2], U8, "plane0", AT_FRAG_SC), 0)]
+        frag_first = carry_scale_rows(placed([P, S], U8, "frag_first", AT_FRAG_SC), 0, staged[:, :S], 0)
         assay_tab.append(tile([P, T2], I32, "frag_sc_listed"))
         nc.sync.dma_start(out=assay_tab[1][:], in_=words(tab2_words, 1))
-        planes.append(carry_scale_rows(placed([P, S + S2], U8, "plane1", AT_FRAG_SC + 2), 1))
+        both_second = carry_scale_rows(placed([P, S + S2], U8, "both_second", AT_FRAG_SC + 2), 4, staged[:], 1)
+        frag_planes = (frag_first, both_second[:, :S])
+        assay_planes = (assay_first, both_second[:, S:])
 
         def gather_frag(a, g):
             nc.vector.tensor_copy(
@@ -127,29 +129,29 @@ def tile_list_fragment_assay_screen_kernel(
                 frag_tab[a][:].bitcast(U32).indirect(frag_list[:, PASS * g // STRIPE : PASS * (g + 1) // STRIPE]),
             )
 
-        def gather_assay(a):
-            for lo, hi in ((0, CHUNK), (CHUNK, 2 * CHUNK), (2 * CHUNK, S2)):
+        def gather_assay(a, cuts):
+            for lo, hi in zip(cuts, cuts[1:]):
                 nc.vector.tensor_copy(
                     assay[a][:, lo:hi],
                     assay_tab[a][:].bitcast(U32).indirect(assay_list[:, lo // STRIPE : hi // STRIPE]),
                 )
 
+        gather_assay(0, (0, S2))
+        wn_raw = placed([P, PACK, N], F32, "wn_raw", AT_ASSAY0)
+        nc.sync.dma_start(out=wn_raw[:], in_=wn.rearrange("(p t) n -> p t n", t=PACK))
         gather_frag(0, 0)
         gather_frag(0, 1)
-        wn_raw = placed([P, PACK, N], F32, "wn_raw", AT_FRAG0)
-        nc.sync.dma_start(out=wn_raw[:], in_=wn.rearrange("(p t) n -> p t n", t=PACK))
+        w4 = placed([P, 2 * N], U8, "w4", AT_FRAG0)
+        nc.sync.dma_start(out=w4[:].bitcast(I32), in_=w4_words[0].bitcast(I32))
         gather_frag(1, 0)
         gather_frag(1, 1)
-        w4 = placed([P, 2 * N], U8, "w4", AT_FRAG1 + 4)
-        nc.sync.dma_start(out=w4[:].bitcast(I32), in_=w4_words[0].bitcast(I32))
         w4_sc = placed([P, N // 4], I32, "w4_sc", AT_FRAG1 + 5)
         for r in range(ROWS):
             nc.sync.dma_start(out=w4_sc[r:P:QUAD, :], in_=w4_scales[0, r:16:ROWS, :].bitcast(I32))
         base_sb = placed([P, N // P], F32, "base_sb", AT_FRAG1 + 6)
         with nc.allow_non_contiguous_dma(reason="one bias value a partition"):
             nc.sync.dma_start(out=base_sb[:], in_=base.rearrange("(r p) -> p r", p=P))
-        gather_assay(0)
-        gather_assay(1)
+        gather_assay(1, (0, P, 2 * CHUNK, S2))
 
         taken = []
 
@@ -157,32 +159,38 @@ def tile_list_fragment_assay_screen_kernel(
             taken.append(psum.tile(shape, F32, name="bank%d" % (len(taken) % TURN)))
             return taken[-1]
 
-        def a_pass(bank, a, c, g, t, joint):
+        def a_pass(dst, a, lo, width, g, t, start, stop):
             col = PASS * g + P * t
             nc.tensor.matmul_mx(
-                out=bank[:, t % 2, :],
+                out=dst,
                 lhsT=frag[a][g][:, P * t : P * t + P].bitcast(FP8X4),
-                lhsT_scale=planes[a][:, col : col + P],
-                rhs=assay[a][:, CHUNK * c : CHUNK * (c + 1)].bitcast(FP8X4),
-                rhs_scale=planes[a][:, S + CHUNK * c : S + CHUNK * (c + 1)],
-                start=(a == 0 and not (joint and t % 2 == 1)),
-                stop=(a == 1 and not (joint and t % 2 == 0)),
+                lhsT_scale=frag_planes[a][:, col : col + P],
+                rhs=assay[a][:, lo : lo + width].bitcast(FP8X4),
+                rhs_scale=assay_planes[a][:, lo : lo + width],
+                start=start,
+                stop=stop,
             )
 
-        def square_unit(k, joint=False):
-            c, g = units[k]
-            banks = [bank_tile([P, 2, CHUNK]) for u in range(2)]
-            for t in range(0, PACK, 1 if joint else 2):
-                a_pass(banks[t // 2], 0, c, g, t, joint)
-            sq = tile([P, 2, CHUNK, 2], F32, "sq%d" % k)
-            for u in range(2):
-                a_pass(banks[u], 1, c, g, 2 * u, joint)
-                if not joint:
-                    a_pass(banks[u], 0, c, g, 2 * u + 1, joint)
-                a_pass(banks[u], 1, c, g, 2 * u + 1, joint)
-                one = ones[k][:, :1] if k in ones else 1.0
+        def square(sq, lo, width, tiles, one, joint):
+            per = BANK // width
+            banks = [bank_tile([P, per, width]) for u in range(2)]
+            for u, (g, t0) in enumerate(tiles):
+                for e in range(per if joint else 1):
+                    a_pass(banks[u][:, e, :], 0, lo, width, g, t0 + e, e == 0, False)
+            for u, (g, t0) in enumerate(tiles):
+                for e in range(per):
+                    if e > 0 and not joint:
+                        a_pass(banks[u][:, e, :], 0, lo, width, g, t0 + e, True, False)
+                    a_pass(banks[u][:, e, :], 1, lo, width, g, t0 + e, False, e == per - 1 or not joint)
                 nc.scalar.activation(sq[:, u], banks[u][:].rearrange("p e n -> p n e"), ACT.Square, bias=one)
             return sq
+
+        def square_unit(k):
+            c, g = units[k]
+            one = ones[k][:, :1] if k in ones else 1.0
+            if k < 2:
+                return square(tile([P, 2, P, PACK], F32, "sq%d" % k), P * k, P, ((0, 0), (1, 0)), one, k < JOINT)
+            return square(tile([P, 2, CHUNK, 2], F32, "sq%d" % k), CHUNK * c, CHUNK, ((g, 0), (g, 2)), one, False)
 
         def z_tile(width, slot):
             return keep.tile([P, width * PACK], BF16, name=slot, align_bytes=64)
@@ -276,9 +284,9 @@ def tile_list_fragment_assay_screen_kernel(
                         )
             queue.dma_start(out=out_tiles[:, r0 : r0 + count, j0 : j0 + width], in_=res[:])
 
-        units = [(c, g) for g in range(2) for c in range(2)] + [(c, g) for c in range(2, 4) for g in range(2)]
+        units = [(0, None), (0, None)] + [(c, g) for c in range(1, 4) for g in range(2)]
         last = len(units) - 1
-        sq = [square_unit(k, joint=k < JOINT) for k in range(AHEAD)]
+        sq = [square_unit(k) for k in range(AHEAD)]
 
         wn_il = keep.tile([P, N * PACK], BF16, name="frag_sc_listed", align_bytes=64)
         wn_dst = wn_il[:].rearrange("p (n t) -> p n t", t=PACK)
@@ -294,17 +302,23 @@ def tile_list_fragment_assay_screen_kernel(
         def quantize_unit(k):
             quantize_z(z[k], *units[k], 0, CHUNK)
 
-        pair = z_tile(2 * CHUNK, "z_pair")
+        z_first3 = z_tile(4 * CHUNK, "z_first")
+        by_g = z_first3[:].rearrange("p (g n t) -> p g n t", g=2, t=PACK)
         z = {}
         for k in range(2):
-            weigh(pair[:, PACK * CHUNK * k : PACK * CHUNK * (k + 1)], sq[k], units[k][1], 0, CHUNK, 0)
+            nc.vector.tensor_tensor(
+                by_g[:, :, P * k : P * (k + 1), :],
+                sq[k][:],
+                fw_ps[:, : 2 * PACK].rearrange("p (g t) -> p g t", g=2).unsqueeze(2).to_broadcast([P, 2, P, PACK]),
+                ALU.mult,
+            )
             sq.append(square_unit(k + AHEAD))
-        z[2] = weigh_unit(2, "z2")
+        weigh(z_first3[:, PACK * CHUNK : 2 * PACK * CHUNK], sq[2], 0, 0, CHUNK, 0)
         sq.append(square_unit(6))
-        quantize_z(pair[:], *units[0], 0, 2 * CHUNK)
+        quantize_z(z_first3[:, : 2 * PACK * CHUNK], 0, 0, 0, 2 * CHUNK)
         z[3] = weigh_unit(3, "sq2")
         sq.append(square_unit(7))
-        quantize_unit(2)
+        quantize_z(z_first3[:, 2 * PACK * CHUNK : 3 * PACK * CHUNK], 0, 1, 0, CHUNK)
         wq = quantize_wn(wn_il)
         quantize_unit(3)
         first = (0, BANK, 1, [bank_tile([P, 1, BANK]) for r in range(N // P)])
@@ -331,8 +345,11 @@ def tile_list_fragment_assay_screen_kernel(
         quantize_z(z_first, c, g, 0, P)
         z_second = weigh(z_tile(P, "z2")[:], sq[last], g, P, P, 0)
         y_sums(third, range(2), wq)
-        y_leave(third, (0, 1), False, nc.sync)
+        for b in range(2):
+            y_leave(third, (b,), False, nc.sync)
         quantize_z(z_second, c, g, P, P)
         y_sums(fourth, (0, 2, 1, 3), wq)
-        y_leave(fourth, (0, 1), True, nc.sync)
-        y_leave(fourth, (2, 3), False, nc.scalar)
+        y_leave(fourth, (0,), True, nc.sync)
+        y_leave(fourth, (2,), False, nc.sync)
+        y_leave(fourth, (1,), True, nc.sync)
+        y_leave(fourth, (3,), False, nc.scalar)

from contextlib import ExitStack

import concourse.mybir as mybir
from concourse.masks import make_identity

K, T, S, T2, S2, N = 1024, 4096, 1024, 2048, 1024, 512
FLOPS = 2 * K * S * S2 + 2 * S * N * S2

F32 = mybir.dt.float32
BF16 = mybir.dt.bfloat16
I32 = mybir.dt.int32
U32 = mybir.dt.uint32
U16 = mybir.dt.uint16
U8 = mybir.dt.uint8
FP8X4 = mybir.dt.float8_e4m3fn_x4
FP4X4 = mybir.dt.float4_e2m1fn_x4
ACT = mybir.ActivationFunctionType
ALU = mybir.AluOpType

P = 128
PACK = 4
PASS = P * PACK
STRIPE = 16
QUAD = 32
ROWS = 4
BANK = 512
CHUNK = 256
LOADED = 96
KIB = 1024
AT_FRAG0, AT_FRAG1, AT_ASSAY0, AT_FRAG_SC, AT_ONES = 0, 17, 34, 42, 47
WN_STEP = 256
SHARE = 80
SHARE_FROM = 3
SHARE_LAST = 32
JOINT = 1
TURN = 7
AHEAD = 4


def tile_list_fragment_assay_screen_kernel(
    tc, tab_words, tab_scales, tab2_words, tab2_scales, offs, offs2, fw, w4_words, w4_scales, wn, base, out
):
    nc = tc.nc
    with ExitStack() as ctx:
        keep = ctx.enter_context(tc.tile_pool(name="keep", bufs=1))
        psum = ctx.enter_context(tc.psum_pool(name="psum", bufs=1))
        held = ctx.enter_context(tc.psum_pool(name="held", bufs=1))

        laid = ctx.enter_context(tc.tile_pool(name="laid", bufs=1))

        def tile(shape, dtype, name):
            return keep.tile(shape, dtype, name=name, align_bytes=64)

        def placed(shape, dtype, name, kib):
            return laid.tile(shape, dtype, name=name, align_bytes=64, offset=kib * KIB)

        frag_list = keep.tile([P, S // STRIPE], U16, name="frag_list")
        assay_list = keep.tile([P, S2 // STRIPE], U16, name="assay_list")
        frag_tab = [placed([P, T], I32, "frag_tab0", AT_FRAG0)]
        assay_tab = [placed([P, T2], I32, "assay_tab0", AT_ASSAY0)]
        frag_tab_sc = placed([P, T // 4], I32, "frag_tab_sc", AT_FRAG_SC)
        assay_tab_sc = placed([P, T2 // 4], I32, "assay_tab_sc", AT_FRAG1 - 1)
        fw_rows = keep.tile([P, PASS], F32, name="fw_rows")
        fw_sb = keep.tile([P, 2 * PACK], F32, name="fw_sb")
        identity = keep.tile([P, P], F32, name="identity")

        nc.gpsimd.memset(fw_rows[:], 0.0)
        make_identity(nc, identity[:])
        nc.vector.memset(assay_tab_sc[:LOADED, :], 0)
        nc.vector.memset(frag_tab_sc[:LOADED, :], 0)

        ones = {k: laid.tile([P, 16], F32, name="one%d" % k, offset=at * KIB - 32) for k, at in ((2, AT_ONES), (3, AT_ONES + 1))}
        for one in ones.values():
            nc.gpsimd.memset(one[:, :1], 1.0)

        def words(tab, a):
            return tab[a].rearrange("p t i -> p (t i)").bitcast(I32)

        for listed, entries, window, rows in (
            (assay_list, offs2, assay_tab_sc, tab2_scales),
            (frag_list, offs, frag_tab_sc, tab_scales),
        ):
            nc.sync.dma_start(listed[:], entries)
            nc.sync.dma_start(out=window[LOADED:, :], in_=rows.rearrange("a q t -> (a q) t").bitcast(I32))
        nc.sync.dma_start(out=assay_tab[0][:], in_=words(tab2_words, 0))
        nc.sync.dma_start(out=frag_tab[0][:], in_=words(tab_words, 0))

        nc.sync.dma_start(out=fw_rows[0:2, :], in_=fw.rearrange("(g i) -> g i", g=2))
        fw_ps = held.tile([P, BANK], F32, name="fw_ps")
        for t in range(PACK):
            nc.tensor.transpose(fw_ps[:, t:BANK:PACK], fw_rows[:, t:PASS:PACK], identity[:])
        nc.scalar.activation(fw_sb[:], fw_ps[:, : 2 * PACK], ACT.Identity)

        frag = [[tile([P, PASS], U32, "frag%d%d" % (a, g)) for g in range(2)] for a in range(2)]
        assay = [tile([P, S2], U32, "assay%d" % a) for a in range(2)]
        frag_sc_listed = tile([P, S], U8, "frag_sc_listed")
        assay_sc_listed = tile([P, S2], U8, "assay_sc_listed")
        staged = tile([P, S + S2], U8, "staged")

        def carry_scale_rows(plane, row, rows, a):
            first = LOADED + 16 * a
            for r in range(ROWS):
                nc.sync.dma_start(
                    out=plane[row + r : P : QUAD, :].bitcast(I32),
                    in_=rows[first + r : first + 16 : ROWS].bitcast(I32),
                )
            return plane[row:, :]

        nc.vector.tensor_copy(assay_sc_listed[:], assay_tab_sc[:].bitcast(U8).indirect(assay_list[:]))
        assay_first = carry_scale_rows(placed([P, S2], U8, "assay_first", AT_FRAG1 - 1), 8, assay_sc_listed[:], 0)
        frag_tab.append(placed([P, T], I32, "frag_tab1", AT_FRAG1))
        nc.sync.dma_start(out=frag_tab[1][:], in_=words(tab_words, 1))
        nc.vector.tensor_copy(frag_sc_listed[:], frag_tab_sc[:].bitcast(U8).indirect(frag_list[:]))
        nc.vector.tensor_copy(staged[:, S:].bitcast(I32), assay_sc_listed[:].bitcast(I32))
        nc.vector.tensor_copy(
            staged[:, :S].rearrange("p (g t m) -> p g t m", g=2, t=PACK),
            frag_sc_listed[:].rearrange("p (g m t) -> p g t m", g=2, t=PACK),
        )
        frag_first = carry_scale_rows(placed([P, S], U8, "frag_first", AT_FRAG_SC), 0, staged[:, :S], 0)
        assay_tab.append(tile([P, T2], I32, "frag_sc_listed"))
        nc.sync.dma_start(out=assay_tab[1][:], in_=words(tab2_words, 1))
        both_second = carry_scale_rows(placed([P, S + S2], U8, "both_second", AT_FRAG_SC + 2), 4, staged[:], 1)
        frag_planes = (frag_first, both_second[:, :S])
        assay_planes = (assay_first, both_second[:, S:])

        def gather_frag(a, g):
            nc.vector.tensor_copy(
                frag[a][g][:].rearrange("p (t m) -> p m t", t=PACK),
                frag_tab[a][:].bitcast(U32).indirect(frag_list[:, PASS * g // STRIPE : PASS * (g + 1) // STRIPE]),
            )

        def gather_assay(a, cuts):
            for lo, hi in zip(cuts, cuts[1:]):
                nc.vector.tensor_copy(
                    assay[a][:, lo:hi],
                    assay_tab[a][:].bitcast(U32).indirect(assay_list[:, lo // STRIPE : hi // STRIPE]),
                )

        gather_assay(0, (0, S2))
        wn_raw = placed([P, PACK, N], F32, "wn_raw", AT_ASSAY0)
        nc.sync.dma_start(out=wn_raw[:], in_=wn.rearrange("(p t) n -> p t n", t=PACK))
        gather_frag(0, 0)
        gather_frag(0, 1)
        w4 = placed([P, 2 * N], U8, "w4", AT_FRAG0)
        nc.sync.dma_start(out=w4[:].bitcast(I32), in_=w4_words[0].bitcast(I32))
        gather_frag(1, 0)
        gather_frag(1, 1)
        w4_sc = placed([P, N // 4], I32, "w4_sc", AT_FRAG1 + 5)
        for r in range(ROWS):
            nc.sync.dma_start(out=w4_sc[r:P:QUAD, :], in_=w4_scales[0, r:16:ROWS, :].bitcast(I32))
        base_sb = placed([P, N // P], F32, "base_sb", AT_FRAG1 + 6)
        with nc.allow_non_contiguous_dma(reason="one bias value a partition"):
            nc.sync.dma_start(out=base_sb[:], in_=base.rearrange("(r p) -> p r", p=P))
        gather_assay(1, (0, P, 2 * CHUNK, S2))

        taken = []

        def bank_tile(shape):
            taken.append(psum.tile(shape, F32, name="bank%d" % (len(taken) % TURN)))
            return taken[-1]

        def a_pass(dst, a, lo, width, g, t, start, stop):
            col = PASS * g + P * t
            nc.tensor.matmul_mx(
                out=dst,
                lhsT=frag[a][g][:, P * t : P * t + P].bitcast(FP8X4),
                lhsT_scale=frag_planes[a][:, col : col + P],
                rhs=assay[a][:, lo : lo + width].bitcast(FP8X4),
                rhs_scale=assay_planes[a][:, lo : lo + width],
                start=start,
                stop=stop,
            )

        def square(sq, lo, width, tiles, one, joint):
            per = BANK // width
            banks = [bank_tile([P, per, width]) for u in range(2)]
            for u, (g, t0) in enumerate(tiles):
                for e in range(per if joint else 1):
                    a_pass(banks[u][:, e, :], 0, lo, width, g, t0 + e, e == 0, False)
            for u, (g, t0) in enumerate(tiles):
                for e in range(per):
                    if e > 0 and not joint:
                        a_pass(banks[u][:, e, :], 0, lo, width, g, t0 + e, True, False)
                    a_pass(banks[u][:, e, :], 1, lo, width, g, t0 + e, False, e == per - 1 or not joint)
                nc.scalar.activation(sq[:, u], banks[u][:].rearrange("p e n -> p n e"), ACT.Square, bias=one)
            return sq

        def square_unit(k):
            c, g = units[k]
            one = ones[k][:, :1] if k in ones else 1.0
            if k < 2:
                return square(tile([P, 2, P, PACK], F32, "sq%d" % k), P * k, P, ((0, 0), (1, 0)), one, k < JOINT)
            return square(tile([P, 2, CHUNK, 2], F32, "sq%d" % k), CHUNK * c, CHUNK, ((g, 0), (g, 2)), one, False)

        def z_tile(width, slot):
            return keep.tile([P, width * PACK], BF16, name=slot, align_bytes=64)

        def weigh(z, sq, g, lo, width, shared):
            own = width - shared
            for engine, weights, n0, n1 in ((nc.vector, fw_ps, 0, own), (nc.gpsimd, fw_sb, own, width)):
                if n1 > n0:
                    engine.tensor_tensor(
                        z[:, PACK * n0 : PACK * n1].rearrange("p (n u e) -> p n u e", u=2, e=2),
                        sq[:, :, lo + n0 : lo + n1, :].rearrange("p u n e -> p n u e"),
                        weights[:, PACK * g : PACK * (g + 1)]
                        .rearrange("p (u e) -> p u e", u=2)
                        .unsqueeze(1)
                        .to_broadcast([P, n1 - n0, 2, 2]),
                        ALU.mult,
                    )
            return z

        zq = {}
        for h in range(2):
            for g in range(2):
                zq[h, g] = (
                    keep.tile([P, BANK], U32, name="z_codes%d%d" % (h, g), align_bytes=64),
                    laid.tile([P, BANK], U8, name="z_scales0%d" % g, align_bytes=64, offset=(AT_ONES + g) * KIB - BANK)
                    if h == 0
                    else tile([P, BANK], U8, "z_scales1%d" % g),
                )

        def quantize_z(z, c, g, lo, width):
            codes, scales = zq[c // 2, g]
            cols = slice(CHUNK * (c % 2) + lo, CHUNK * (c % 2) + lo + width)
            nc.vector.quantize_mx(out=codes[:, cols].bitcast(FP8X4), scales=scales[:, cols], in_=z)

        def quantize_wn(wn_il):
            codes = keep.tile([P, N], U32, name="wn_codes", align_bytes=64)
            scales = placed([P, N], U8, "wn_scales", AT_ONES + 1)
            nc.vector.quantize_mx(out=codes[:].bitcast(FP8X4), scales=scales[:], in_=wn_il[:])
            return codes, scales

        def y_pass(dst, g, r, h, cols, wq, start):
            if g == 0:
                lhsT = w4[:, 2 * P * r : 2 * P * (r + 1)].bitcast(FP4X4)
                lhsT_scale = w4_sc[:].bitcast(U8)[:, P * r : P * (r + 1)]
            else:
                lhsT = wq[0][:, P * r : P * (r + 1)].bitcast(FP8X4)
                lhsT_scale = wq[1][:, P * r : P * (r + 1)]
            nc.tensor.matmul_mx(
                out=dst,
                lhsT=lhsT,
                lhsT_scale=lhsT_scale,
                rhs=zq[h, g][0][:, cols].bitcast(FP8X4),
                rhs_scale=zq[h, g][1][:, cols],
                start=start and g == 0,
                stop=start and g == 1,
            )

        out_tiles = out.rearrange("(r p) j -> p r j", p=P)

        def y_open(j0, width, per_bank):
            h, off = divmod(j0, BANK)
            step = BANK if width == BANK else P
            banks = [bank_tile([P, per_bank, width]) for b in range(N // P // per_bank)]
            for r in range(N // P):
                for s in range(0, width, step):
                    dst = banks[r // per_bank][:, r % per_bank, s : s + step]
                    y_pass(dst, 0, r, h, slice(off + s, off + s + step), None, r % per_bank == 0 and s == 0)
            return j0, width, per_bank, banks

        def y_sums(block, which, wq):
            j0, width, per_bank, banks = block
            h, off = divmod(j0, BANK)
            for b in which:
                for e in range(per_bank):
                    y_pass(banks[b][:, e, :], 1, per_bank * b + e, h, slice(off, off + width), wq, e == per_bank - 1)

        def y_leave(block, which, on_vector, queue, slot=None):
            j0, width, per_bank, banks = block
            r0, count = per_bank * which[0], per_bank * len(which)
            res = keep.tile([P, count, width], F32, name=slot or "res%d_%d" % (j0, r0), align_bytes=64)
            for i, b in enumerate(which):
                rows = slice(per_bank * b, per_bank * (b + 1))
                if on_vector:
                    bias = base_sb[:, rows].unsqueeze(2).to_broadcast([P, per_bank, width])
                    nc.vector.tensor_tensor(res[:, per_bank * i : per_bank * (i + 1), :], banks[b][:], bias, ALU.add)
                else:
                    for e in range(per_bank):
                        r = rows.start + e
                        nc.scalar.activation(
                            res[:, r - r0, :], banks[b][:, e, :], ACT.Identity, bias=base_sb[:, r : r + 1]
                        )
            queue.dma_start(out=out_tiles[:, r0 : r0 + count, j0 : j0 + width], in_=res[:])

        units = [(0, None), (0, None)] + [(c, g) for c in range(1, 4) for g in range(2)]
        last = len(units) - 1
        sq = [square_unit(k) for k in range(AHEAD)]

        wn_il = keep.tile([P, N * PACK], BF16, name="frag_sc_listed", align_bytes=64)
        wn_dst = wn_il[:].rearrange("p (n t) -> p n t", t=PACK)
        wn_src = wn_raw[:].rearrange("p t n -> p n t")
        for n0 in range(0, N, WN_STEP):
            cols = slice(n0, n0 + WN_STEP)
            nc.gpsimd.tensor_scalar(wn_dst[:, cols], wn_src[:, cols], 1.0, 0.0, ALU.mult, ALU.add)

        def weigh_unit(k, slot):
            dst = z_tile(CHUNK, slot)[:]
            return weigh(dst, sq[k], units[k][1], 0, CHUNK, SHARE if k >= SHARE_FROM else 0)

        def quantize_unit(k):
            quantize_z(z[k], *units[k], 0, CHUNK)

        z_first3 = z_tile(4 * CHUNK, "z_first")
        by_g = z_first3[:].rearrange("p (g n t) -> p g n t", g=2, t=PACK)
        z = {}
        for k in range(2):
            nc.vector.tensor_tensor(
                by_g[:, :, P * k : P * (k + 1), :],
                sq[k][:],
                fw_ps[:, : 2 * PACK].rearrange("p (g t) -> p g t", g=2).unsqueeze(2).to_broadcast([P, 2, P, PACK]),
                ALU.mult,
            )
            sq.append(square_unit(k + AHEAD))
        weigh(z_first3[:, PACK * CHUNK : 2 * PACK * CHUNK], sq[2], 0, 0, CHUNK, 0)
        sq.append(square_unit(6))
        quantize_z(z_first3[:, : 2 * PACK * CHUNK], 0, 0, 0, 2 * CHUNK)
        z[3] = weigh_unit(3, "sq2")
        sq.append(square_unit(7))
        quantize_z(z_first3[:, 2 * PACK * CHUNK : 3 * PACK * CHUNK], 0, 1, 0, CHUNK)
        wq = quantize_wn(wn_il)
        quantize_unit(3)
        first = (0, BANK, 1, [bank_tile([P, 1, BANK]) for r in range(N // P)])
        for r in range(N // P):
            for e in range(2):
                y_pass(first[3][r][:, 0, :], e, r, 0, slice(0, BANK), wq, True)
        z[4] = weigh_unit(4, "frag_sc_listed")
        for b in range(4):
            y_leave(first, (b,), False, nc.sync)
        z[5] = weigh_unit(5, "sq2")
        quantize_unit(4)
        second = y_open(2 * CHUNK, CHUNK, 1)
        z[6] = weigh_unit(6, "sq5")
        quantize_unit(5)
        y_sums(second, range(4), wq)
        y_leave(second, (0, 1), False, nc.sync)
        y_leave(second, (2, 3), False, nc.sync)

        c, g = units[last]
        z_first = weigh(z_tile(P, "sq6")[:], sq[last], g, 0, P, SHARE_LAST)
        quantize_unit(last - 1)
        third = y_open(c * CHUNK, P, 2)
        fourth = y_open(c * CHUNK + P, P, 1)
        quantize_z(z_first, c, g, 0, P)
        z_second = weigh(z_tile(P, "z2")[:], sq[last], g, P, P, 0)
        y_sums(third, range(2), wq)
        for b in range(2):
            y_leave(third, (b,), False, nc.sync)
        quantize_z(z_second, c, g, P, P)
        y_sums(fourth, (0, 2, 1, 3), wq)
        y_leave(fourth, (0,), True, nc.sync)
        y_leave(fourth, (2,), False, nc.sync)
        y_leave(fourth, (1,), True, nc.sync)
        y_leave(fourth, (3,), False, nc.scalar)
